import numpy as np
import ml_dtypes


def mxq(x, axis, fmt="e4m3"):
    dtype, down = {"e4m3": (ml_dtypes.float8_e4m3fn, 7), "e5m2": (ml_dtypes.float8_e5m2, 14)}[fmt]
    v = np.moveaxis(np.asarray(x, np.float32).astype(ml_dtypes.bfloat16).astype(np.float64), axis, -1)
    blocks = v.reshape(v.shape[:-1] + (-1, 32))
    amax = np.abs(blocks).max(-1, keepdims=True)
    byte = np.maximum(np.where(amax > 0, np.frexp(amax)[1] - 1 + 127, 0) - down, 1)
    scale = np.exp2(byte - 127.0)
    codes = (blocks / scale).astype(np.float32).astype(dtype).astype(np.float64)
    return np.moveaxis((codes * scale).reshape(v.shape), -1, axis)


WIDE = False


def mx_kscale(k):
    if not WIDE:
        return np.ones(k)
    levels = np.array([10, -10, 5, -5, 0])
    if k % 512:
        return np.exp2(np.random.permutation(np.resize(levels, k // 32))).repeat(32)
    a = np.empty((k // 512, 16))
    for p in range(k // 512):
        a[p, :8] = np.random.permutation(np.resize(levels, 8))
        for g in range(8):
            far = levels[np.abs(levels - a[p, g]) >= 10]
            a[p, g + 8] = far[np.random.randint(len(far))]
    return np.exp2(a.ravel()).repeat(32)


def f64(x):
    return np.asarray(x).astype(np.float64)


def striped(idx):
    return np.tile(idx.reshape(-1, 16).T, (8, 1)).astype(np.uint16)


def unstriped(offs):
    return offs[:16].T.reshape(-1).astype(np.int64)


def pack_weight(w):
    k, n = w.shape
    w = f64(np.asarray(w, np.float32).astype(ml_dtypes.bfloat16)).reshape(k // 32, 32, n)
    amax = np.abs(w).max(1)
    byte = np.clip(np.where(amax > 0, np.frexp(amax)[1] - 1 + 127 - 7, 1), 1, 254)
    scaled = (w * np.exp2(127.0 - byte)[:, None, :]).reshape(k, n).astype(np.float32)
    words = np.ascontiguousarray(scaled.reshape(k // 512, 128, 4, n).transpose(0, 1, 3, 2)).astype(ml_dtypes.float8_e4m3fn).view(np.uint8)
    return words, np.ascontiguousarray(byte.astype(np.uint8).reshape(k // 512, 16, n))


def unpack_weight(words, scales):
    g, p, n, _ = words.shape
    vals = np.ascontiguousarray(words).view(ml_dtypes.float8_e4m3fn).astype(np.float64) * np.repeat(np.exp2(scales.astype(np.float64) - 127.0), 8, axis=1)[..., None]
    return vals.transpose(0, 1, 3, 2).reshape(g * 512, n)


def gelu(v):
    return 0.5 * v * (1.0 + np.tanh(np.sqrt(2.0 / np.pi) * (v + 0.044715 * v**3)))


K, T, S, H, N, U = 1024, 2048, 512, 512, 128, 1024


def setup_inputs():
    n = np.random.standard_normal
    s = mx_kscale(K)[:, None]
    u = mx_kscale(H)
    packed_xT = pack_weight(n((K, T)) * s)
    return {
        "x_words": packed_xT[0],
        "x_scales": packed_xT[1],
        "w1": (n((K, H)) / np.sqrt(K) / s * u).astype(np.float32),
        "w2": (n((H, N)) / np.sqrt(H) / u[:, None]).astype(np.float32),
        "skip": (n((H, U)) * u[:, None]).astype(np.float32),
        "offs": striped(np.random.permutation(T)[:S]),
        "cell": striped(np.random.permutation(U)[:S]),
    }


def reference(x_words, x_scales, w1, w2, skip, offs, cell):
    xq = unpack_weight(x_words, x_scales)[:, unstriped(offs)]
    up = np.zeros((H, U))
    up[:, unstriped(cell)] = gelu(mxq(f64(w1), 0, "e4m3").T @ xq)
    z = up + f64(skip)
    return mxq(f64(w2), 0, "e4m3").T @ mxq(z, 0, "e4m3")

@@ -1,0 +1,250 @@
+from contextlib import ExitStack
+
+import concourse.mybir as mybir
+from concourse.masks import make_identity
+
+K, T, S, H, N, U = 1024, 2048, 512, 512, 128, 1024
+FLOPS = 2 * K * H * S + 2 * H * N * U
+
+F32 = mybir.dt.float32
+BF16 = mybir.dt.bfloat16
+I32 = mybir.dt.int32
+U32 = mybir.dt.uint32
+U16 = mybir.dt.uint16
+U8 = mybir.dt.uint8
+FP8X4 = mybir.dt.float8_e4m3fn_x4
+GELU = mybir.ActivationFunctionType.Gelu_apprx_tanh
+
+P = 128
+HALF_S = S // 2
+HALF_COLS = HALF_S // 16
+
+
+def tile_picked_unet_gelu_p_kernel(
+    tc, x_words, x_scales, w1, w2, skip, offs, cell, out
+):
+    nc = tc.nc
+    with ExitStack() as ctx:
+        sb = ctx.enter_context(tc.tile_pool(name="sb", bufs=1))
+        ps = ctx.enter_context(tc.psum_pool(name="ps", bufs=1))
+
+        def tile(shape, dtype, name):
+            return sb.tile(shape, dtype, name=name, align_bytes=64)
+
+        offs_sb = tile([P, S // 16], U16, "offs_sb")
+        cell_sb = tile([P, S // 16], U16, "cell_sb")
+        nc.sync.dma_start(offs_sb[:], offs)
+        nc.sync.dma_start(cell_sb[:], cell)
+
+        xs = tile([P, T], U8, "xs")
+        nc.gpsimd.memset(xs[:].bitcast(I32), 0)
+        for q in range(4):
+            nc.scalar.dma_start(
+                xs[32 * q : 32 * q + 8, :].bitcast(I32),
+                x_scales[:, 4 * q : 4 * q + 4, :].bitcast(I32),
+            )
+        warm = tile([P, 8], F32, "warm")
+        warm_out = tile([P, 8], F32, "warm_out")
+        nc.vector.memset(warm[:], 0.0)
+        nc.scalar.activation(warm_out[:], warm[:], GELU)
+
+        def load_w1(c0, width, name):
+            raws = []
+            for g in range(2):
+                raw = tile([P, 4, width], F32, f"{name}{g}")
+                nc.sync.dma_start(
+                    raw[:], w1[512 * g : 512 * (g + 1), c0 : c0 + width].rearrange("(p j) c -> p j c", j=4)
+                )
+                raws.append(raw)
+            return raws
+
+        raw0 = load_w1(0, P, "raw0_")
+        xw = []
+        for g in range(2):
+            words = tile([P, T], I32, f"xw{g}")
+            nc.sync.dma_start(words[:], x_words[g].rearrange("p n t -> p (n t)").bitcast(I32))
+            xw.append(words)
+        raw1 = load_w1(P, P, "raw1_")
+        rawb = load_w1(2 * P, 2 * P, "rawb_")
+        skip_sb = []
+        w2_raw = tile([P, 2, 4, N], F32, "w2_raw")
+        for t in range(4):
+            if t == 2:
+                for half in range(2):
+                    nc.sync.dma_start(
+                        w2_raw[64 * half : 64 * (half + 1)].rearrange("p a s n -> p a (s n)"),
+                        w2.rearrange("(a p s) n -> p a (s n)", a=2, s=4),
+                    )
+            rows = tile([P, U], F32, f"skip{t}")
+            if t < 2:
+                nc.sync.dma_start(rows[:], skip[P * t : P * (t + 1), :])
+            else:
+                nc.sync.dma_start(
+                    rows[:], skip[2 * P :, :].rearrange("(q u e) v -> u q e v", u=2, e=2)[t - 2]
+                )
+            skip_sb.append(rows)
+
+        ident = tile([P, P], F32, "ident")
+        make_identity(nc, ident[:])
+        w2_bf = tile([P, 2, 2, N, 4], BF16, "w2_bf")
+        nc.gpsimd.memset(w2_bf[:].rearrange("p h a n s -> p (h a n s)").bitcast(I32), 0)
+
+        up = []
+        for t in range(4):
+            window = tile([P, U], F32, f"up{t}")
+            nc.vector.memset(window[:], 0.0)
+            up.append(window)
+
+        def quantize(src, name):
+            width = src.shape[1] // 4
+            codes = tile([P, width], U32, name + "_codes")
+            scales = tile([P, width], U8, name + "_scales")
+            nc.vector.quantize_mx(out=codes[:].bitcast(FP8X4), scales=scales[:], in_=src)
+            return codes, scales
+
+        def cast_w1(raws, name):
+            grouped = tile([P, 2, P, 4], BF16, name)
+            for g in range(2):
+                nc.scalar.copy(
+                    grouped[:, g].rearrange("p (c i) j -> p c j i", i=4),
+                    raws[g][:].rearrange("p j (c i) -> p c j i", i=4),
+                )
+            return quantize(grouped[:].rearrange("p g c j -> p (g c j)"), name)
+
+        wq0 = cast_w1(raw0, "wb0")
+
+        xg_scales = tile([P, S], U8, "xg_scales")
+        nc.vector.tensor_copy(xg_scales[:], xs[:].indirect(offs_sb[:]))
+        xg0 = tile([P, S], U32, "xg0")
+        nc.vector.tensor_copy(xg0[:], xw[0][:].bitcast(U32).indirect(offs_sb[:]))
+        xg1 = tile([P, S], U32, "xg1")
+        for part in range(2):
+            nc.vector.tensor_copy(
+                xg1[:, HALF_S * part : HALF_S * (part + 1)],
+                xw[1][:].bitcast(U32).indirect(offs_sb[:, HALF_COLS * part : HALF_COLS * (part + 1)]),
+            )
+        xg = [xg0, xg1]
+
+        def first_product(bank, wq, col0, *bounds):
+            codes, scales = wq
+            acc = ps.tile([P, bounds[-1] - bounds[0]], F32, name=f"back{bank}", tag=f"back{bank}")
+            for lo, hi in zip(bounds, bounds[1:]):
+                for g in range(2):
+                    cols = slice(col0 + P * g, col0 + P * (g + 1))
+                    nc.tensor.matmul_mx(
+                        acc[:, lo - bounds[0] : hi - bounds[0]],
+                        lhsT=codes[:, cols].bitcast(FP8X4),
+                        lhsT_scale=scales[:, cols],
+                        rhs=xg[g][:, lo:hi].bitcast(FP8X4),
+                        rhs_scale=xg_scales[4 * g :, lo:hi],
+                        start=(g == 0),
+                        stop=(g == 1),
+                    )
+            return acc
+
+        def gelu_scatter(t, acc, h_sb, offsets):
+            nc.scalar.activation(h_sb, acc, GELU)
+            nc.vector.tensor_copy(up[t][:].indirect(offsets), h_sb)
+
+        cell_first, cell_second = cell_sb[:, :HALF_COLS], cell_sb[:, HALF_COLS:]
+
+        acc0a = first_product(0, wq0, 0, 0, HALF_S)
+        acc0b = first_product(1, wq0, 0, HALF_S, S)
+        h0a = tile([P, HALF_S], F32, "h0a")
+        gelu_scatter(0, acc0a[:], h0a[:], cell_first)
+        wq1 = cast_w1(raw1, "wb1")
+        gelu_scatter(0, acc0b[:], raw1[1][:].rearrange("p j c -> p (j c)")[:, :HALF_S], cell_second)
+
+        acc1a = first_product(2, wq1, 0, 0, P)
+        acc1b = first_product(3, wq1, 0, P, 2 * P, S)
+        h1a = tile([P, P], F32, "h1a")
+        gelu_scatter(1, acc1a[:], h1a[:], cell_sb[:, : P // 16])
+        wbb = tile([P, 2, 2, P, 4], BF16, "wbb")
+        for g in range(2):
+            nc.scalar.copy(
+                wbb[:, :, g].rearrange("p u (q e) j -> p u q j e", e=2),
+                rawb[g][:].rearrange("p j (q u e) -> p u q j e", u=2, e=2),
+            )
+        wqb = quantize(wbb[:].rearrange("p u g c j -> p (u g c j)"), "wbb")
+        gelu_scatter(1, acc1b[:], rawb[1][:].rearrange("p j c -> p (j c)")[:, : S - P], cell_sb[:, P // 16 :])
+
+        for u in range(2):
+            acc = first_product(u, wqb, 2 * P * u, 0, S)
+            h_sb = tile([P, S], F32, f"h{2 + u}")
+            gelu_scatter(2 + u, acc[:], h_sb[:], cell_sb[:])
+
+        def turn_and_add(t):
+            banks = [ps.tile([P, 2, P], F32, name=f"turned{j}", tag=f"turned{j}") for j in range(4)]
+            for src in (skip_sb[t], up[t]):
+                for j in range(4):
+                    for half in range(2):
+                        v0 = 512 * half + P * j
+                        nc.tensor.matmul(
+                            banks[j][:, half, :],
+                            lhsT=src[:, v0 : v0 + P],
+                            rhs=ident[:],
+                            is_transpose=True,
+                            start=(src is skip_sb[t] and half == 0),
+                            stop=(src is up[t] and half == 1),
+                        )
+            return banks
+
+        def back_banks():
+            return [ps.tile([P, 2, P], F32, name=f"back{j}", tag=f"back{j}") for j in range(4)]
+
+        def weave(copy, zq, back):
+            copy(zq.bitcast(F32).rearrange("p (v u) -> p v u", u=2), back[:].rearrange("p u v -> p v u"))
+
+        zt_a = [tile([P, 2, 2, P], BF16, f"zt_a{j}") for j in range(4)]
+        for t in range(2):
+            for j, bank in enumerate(turn_and_add(t)):
+                nc.scalar.copy(
+                    zt_a[j][:, :, :, 64 * t : 64 * (t + 1)].rearrange("p u h (q e) -> p h u q e", e=2),
+                    bank[:].rearrange("p h (q u e) -> p h u q e", u=2, e=2),
+                )
+        zq_a = tile([P, 2 * U], BF16, "zq_a")
+        for j, back in enumerate(back_banks()):
+            for u in range(2):
+                nc.tensor.transpose(back[:, u, :], zt_a[j][:, u].rearrange("p h c -> p (h c)").bitcast(F32), ident[:])
+            weave(nc.scalar.copy, zq_a[:, 512 * j : 512 * (j + 1)], back)
+
+        for half in range(2):
+            rows = slice(64 * half, 64 * (half + 1))
+            nc.scalar.copy(
+                w2_bf[rows, half].rearrange("p a (c i) s -> p a c s i", i=4),
+                w2_raw[rows].rearrange("p a s (c i) -> p a c s i", i=4),
+            )
+
+        backs = back_banks()
+        for u in range(2):
+            for j, bank in enumerate(turn_and_add(2 + u)):
+                zt = tile([P, 2 * P], BF16, f"zt_b{u}{j}")
+                copy = nc.vector.tensor_copy if (u, j) == (1, 3) else nc.scalar.copy
+                copy(zt[:], bank[:].rearrange("p h c -> p (h c)"))
+                nc.tensor.transpose(backs[j][:, u, :], zt[:].bitcast(F32), ident[:])
+
+        w2_codes, w2_scales = quantize(w2_bf[:].rearrange("p h a n s -> p (h a n s)"), "w2q")
+        za = quantize(zq_a[:], "za")
+
+        out_view = out.rearrange("m (h j c) -> m j h c", h=2, j=4)
+        for j in range(4):
+            zq_b = tile([P, 4 * P], BF16, f"zq_b{j}")
+            weave(nc.scalar.copy, zq_b[:], backs[j])
+            zb = quantize(zq_b[:], f"zb{j}")
+            acc = ps.tile([P, 2, P], F32, name=f"turned{j}", tag=f"turned{j}")
+            for a, (codes, scales, cols) in enumerate((za + (slice(P * j, P * (j + 1)),), zb + (slice(0, P),))):
+                for half in range(2):
+                    w_cols = slice(N * (2 * half + a), N * (2 * half + a + 1))
+                    nc.tensor.matmul_mx(
+                        acc[:, half, :],
+                        lhsT=w2_codes[:, w_cols].bitcast(FP8X4),
+                        lhsT_scale=w2_scales[:, w_cols],
+                        rhs=codes[:, cols].bitcast(FP8X4),
+                        rhs_scale=scales[:, cols],
+                        start=(a == 0 and half == 0),
+                        stop=(a == 1 and half == 1),
+                    )
+            result = tile([P, 2, P], F32, f"result{j}")
+            copy = nc.scalar.copy if j % 2 == 0 else nc.vector.tensor_copy
+            copy(result[:], acc[:])
+            nc.sync.dma_start(out_view[:, j], result[:])

@@ -69,7 +69,7 @@ def tile_picked_unet_gelu_p_kernel(
         skip_sb = []
         w2_raw = tile([P, 2, 4, N], F32, "w2_raw")
         for t in range(4):
-            if t == 2:
+            if t == 3:
                 for half in range(2):
                     nc.sync.dma_start(
                         w2_raw[64 * half : 64 * (half + 1)].rearrange("p a s n -> p a (s n)"),
@@ -86,14 +86,14 @@ def tile_picked_unet_gelu_p_kernel(
 
         ident = tile([P, P], F32, "ident")
         make_identity(nc, ident[:])
-        w2_bf = tile([P, 2, 2, N, 4], BF16, "w2_bf")
-        nc.gpsimd.memset(w2_bf[:].rearrange("p h a n s -> p (h a n s)").bitcast(I32), 0)
 
         up = []
         for t in range(4):
             window = tile([P, U], F32, f"up{t}")
             nc.vector.memset(window[:], 0.0)
             up.append(window)
+        w2_codes = tile([P, 2, 2 * N], U32, "w2_codes")
+        nc.vector.memset(w2_codes[:].bitcast(I32), 0)
 
         def quantize(src, name):
             width = src.shape[1] // 4
@@ -173,71 +173,80 @@ def tile_picked_unet_gelu_p_kernel(
             h_sb = tile([P, S], F32, f"h{2 + u}")
             gelu_scatter(2 + u, acc[:], h_sb[:], cell_sb[:])
 
-        def turn_and_add(t):
-            banks = [ps.tile([P, 2, P], F32, name=f"turned{j}", tag=f"turned{j}") for j in range(4)]
+        def turn_and_add(t, tags):
+            pairs = 4 // len(tags)
+            banks = [ps.tile([P, pairs, 2, P], F32, name=tag, tag=tag) for tag in tags]
             for src in (skip_sb[t], up[t]):
                 for j in range(4):
                     for half in range(2):
                         v0 = 512 * half + P * j
                         nc.tensor.matmul(
-                            banks[j][:, half, :],
+                            banks[j // pairs][:, j % pairs, half, :],
                             lhsT=src[:, v0 : v0 + P],
                             rhs=ident[:],
                             is_transpose=True,
-                            start=(src is skip_sb[t] and half == 0),
-                            stop=(src is up[t] and half == 1),
+                            start=(src is skip_sb[t] and j % pairs == 0 and half == 0),
+                            stop=(src is up[t] and j % pairs == pairs - 1 and half == 1),
                         )
             return banks
 
-        def back_banks():
-            return [ps.tile([P, 2, P], F32, name=f"back{j}", tag=f"back{j}") for j in range(4)]
-
-        def weave(copy, zq, back):
-            copy(zq.bitcast(F32).rearrange("p (v u) -> p v u", u=2), back[:].rearrange("p u v -> p v u"))
-
-        zt_a = [tile([P, 2, 2, P], BF16, f"zt_a{j}") for j in range(4)]
+        zt_a = [tile([P, 2, 4, P], BF16, f"zt_a{jj}") for jj in range(2)]
         for t in range(2):
-            for j, bank in enumerate(turn_and_add(t)):
+            for jj, bank in enumerate(turn_and_add(t, (f"turned{2 * t}", f"turned{2 * t + 1}"))):
                 nc.scalar.copy(
-                    zt_a[j][:, :, :, 64 * t : 64 * (t + 1)].rearrange("p u h (q e) -> p h u q e", e=2),
-                    bank[:].rearrange("p h (q u e) -> p h u q e", u=2, e=2),
+                    zt_a[jj][:, :, :, 64 * t : 64 * (t + 1)].rearrange("p u b (q e) -> p b u q e", e=2),
+                    bank[:].rearrange("p j h (q u e) -> p (j h) u q e", u=2, e=2),
                 )
         zq_a = tile([P, 2 * U], BF16, "zq_a")
-        for j, back in enumerate(back_banks()):
-            for u in range(2):
-                nc.tensor.transpose(back[:, u, :], zt_a[j][:, u].rearrange("p h c -> p (h c)").bitcast(F32), ident[:])
-            weave(nc.scalar.copy, zq_a[:, 512 * j : 512 * (j + 1)], back)
-
-        for half in range(2):
-            rows = slice(64 * half, 64 * (half + 1))
+        for jj in range(2):
+            back = ps.tile([P, 2, 2, P], F32, name=f"back{jj}", tag=f"back{jj}")
+            for j in range(2):
+                for u in range(2):
+                    words = zt_a[jj][:, u, 2 * j : 2 * j + 2, :].rearrange("p h c -> p (h c)").bitcast(F32)
+                    nc.tensor.transpose(back[:, j, u, :], words, ident[:])
             nc.scalar.copy(
-                w2_bf[rows, half].rearrange("p a (c i) s -> p a c s i", i=4),
-                w2_raw[rows].rearrange("p a s (c i) -> p a c s i", i=4),
+                zq_a[:, U * jj : U * (jj + 1)].bitcast(F32).rearrange("p (j v u) -> p j v u", j=2, u=2),
+                back[:].rearrange("p j u v -> p j v u"),
             )
 
-        backs = back_banks()
-        for u in range(2):
-            for j, bank in enumerate(turn_and_add(2 + u)):
-                zt = tile([P, 2 * P], BF16, f"zt_b{u}{j}")
-                copy = nc.vector.tensor_copy if (u, j) == (1, 3) else nc.scalar.copy
-                copy(zt[:], bank[:].rearrange("p h c -> p (h c)"))
-                nc.tensor.transpose(backs[j][:, u, :], zt[:].bitcast(F32), ident[:])
+        w2_bf = tile([P, 2, N, 4], BF16, "w2_bf")
+        nc.scalar.copy(
+            w2_bf[:].rearrange("p a (c i) s -> p a c s i", i=4),
+            w2_raw[:].rearrange("p a s (c i) -> p a c s i", i=4),
+        )
 
-        w2_codes, w2_scales = quantize(w2_bf[:].rearrange("p h a n s -> p (h a n s)"), "w2q")
+        zt_low = [tile([P, 2, 2 * P], BF16, f"zt_low{jj}") for jj in range(2)]
+        for jj, bank in enumerate(turn_and_add(2, ("back2", "back3"))):
+            nc.scalar.copy(zt_low[jj][:], bank[:].rearrange("p j h c -> p j (h c)"))
+        backs = [ps.tile([P, 2, P], F32, name=f"back{j}", tag=f"back{j}") for j in range(4)]
+        for j in range(4):
+            nc.tensor.transpose(backs[j][:, 0, :], zt_low[j // 2][:, j % 2, :].bitcast(F32), ident[:])
+        for j, bank in enumerate(turn_and_add(3, [f"turned{j}" for j in range(4)])):
+            zt_high = tile([P, 2 * P], BF16, f"zt_high{j}")
+            copy = nc.vector.tensor_copy if j == 3 else nc.scalar.copy
+            copy(zt_high[:], bank[:].rearrange("p j h c -> p (j h c)"))
+            nc.tensor.transpose(backs[j][:, 1, :], zt_high[:].bitcast(F32), ident[:])
+
+        w2_both, w2_scales = quantize(w2_bf[:].rearrange("p a n s -> p (a n s)"), "w2q")
+        for half in range(2):
+            rows = slice(64 * half, 64 * (half + 1))
+            nc.vector.tensor_copy(w2_codes[rows, half, :], w2_both[rows, :])
         za = quantize(zq_a[:], "za")
 
         out_view = out.rearrange("m (h j c) -> m j h c", h=2, j=4)
         for j in range(4):
             zq_b = tile([P, 4 * P], BF16, f"zq_b{j}")
-            weave(nc.scalar.copy, zq_b[:], backs[j])
+            nc.scalar.copy(
+                zq_b[:].bitcast(F32).rearrange("p (v u) -> p v u", u=2), backs[j][:].rearrange("p u v -> p v u")
+            )
             zb = quantize(zq_b[:], f"zb{j}")
             acc = ps.tile([P, 2, P], F32, name=f"turned{j}", tag=f"turned{j}")
             for a, (codes, scales, cols) in enumerate((za + (slice(P * j, P * (j + 1)),), zb + (slice(0, P),))):
+                w_cols = slice(N * a, N * (a + 1))
                 for half in range(2):
-                    w_cols = slice(N * (2 * half + a), N * (2 * half + a + 1))
                     nc.tensor.matmul_mx(
                         acc[:, half, :],
-                        lhsT=w2_codes[:, w_cols].bitcast(FP8X4),
+                        lhsT=w2_codes[:, half, w_cols].bitcast(FP8X4),
                         lhsT_scale=w2_scales[:, w_cols],
                         rhs=codes[:, cols].bitcast(FP8X4),
                         rhs_scale=scales[:, cols],

@@ -1,7 +1,6 @@
 from contextlib import ExitStack
 
 import concourse.mybir as mybir
-from concourse.masks import make_identity
 
 K, T, S, H, N, U = 1024, 2048, 512, 512, 128, 1024
 FLOPS = 2 * K * H * S + 2 * H * N * U
@@ -16,8 +15,13 @@ FP8X4 = mybir.dt.float8_e4m3fn_x4
 GELU = mybir.ActivationFunctionType.Gelu_apprx_tanh
 
 P = 128
+HALF_P = P // 2
+K_PASS = 4 * P
+HALF_U = U // 2
+STRIPES = HALF_U // P
+LIST_ROWS = 16
 HALF_S = S // 2
-HALF_COLS = HALF_S // 16
+HEAD_S = 128
 
 
 def tile_picked_unet_gelu_p_kernel(
@@ -28,70 +32,83 @@ def tile_picked_unet_gelu_p_kernel(
         sb = ctx.enter_context(tc.tile_pool(name="sb", bufs=1))
         ps = ctx.enter_context(tc.psum_pool(name="ps", bufs=1))
 
-        def tile(shape, dtype, name):
-            return sb.tile(shape, dtype, name=name, align_bytes=64)
+        def tile(shape, dtype, name, pool=sb):
+            return pool.tile(shape, dtype, name=name, align_bytes=64)
 
-        offs_sb = tile([P, S // 16], U16, "offs_sb")
-        cell_sb = tile([P, S // 16], U16, "cell_sb")
+        def psum(shape, tag):
+            return ps.tile(shape, F32, name=tag, tag=tag)
+
+        def entries(list_sb, lo, hi):
+            return list_sb[:, lo // LIST_ROWS : hi // LIST_ROWS]
+
+        offs_sb = tile([P, S // LIST_ROWS], U16, "offs_sb")
+        cell_sb = tile([P, S // LIST_ROWS], U16, "cell_sb")
         nc.sync.dma_start(offs_sb[:], offs)
         nc.sync.dma_start(cell_sb[:], cell)
 
-        xs = tile([P, T], U8, "xs")
-        nc.gpsimd.memset(xs[:].bitcast(I32), 0)
+        def load_words(g, pool):
+            words = tile([P, T], I32, f"x_words{g}", pool)
+            nc.sync.dma_start(words[:], x_words[g].rearrange("p n s -> p (n s)").bitcast(I32))
+            return words
+
+        x_words_sb = [load_words(0, sb)]
+
+        x_scales_sb = tile([P, T], U8, "x_scales_sb")
+        nc.vector.memset(x_scales_sb[:].bitcast(I32), 0)
         for q in range(4):
-            nc.scalar.dma_start(
-                xs[32 * q : 32 * q + 8, :].bitcast(I32),
+            nc.sync.dma_start(
+                x_scales_sb[32 * q : 32 * q + 8, :].bitcast(I32),
                 x_scales[:, 4 * q : 4 * q + 4, :].bitcast(I32),
             )
-        warm = tile([P, 8], F32, "warm")
-        warm_out = tile([P, 8], F32, "warm_out")
-        nc.vector.memset(warm[:], 0.0)
-        nc.scalar.activation(warm_out[:], warm[:], GELU)
+
+        ident = tile([P, P], F32, "ident")
+        with tc.tile_pool(name="early", bufs=1) as early:
+            ones = tile([P, P], F32, "ones", early)
+            nc.gpsimd.memset(ones[:], 1.0)
+            nc.gpsimd.affine_select(
+                out=ident[:],
+                in_=ones[:],
+                compare_op=mybir.AluOpType.is_equal,
+                fill=0.0,
+                base=0,
+                pattern=[[-1, P]],
+                channel_multiplier=1,
+            )
+        late = ctx.enter_context(tc.tile_pool(name="late", bufs=1))
 
         def load_w1(c0, width, name):
             raws = []
             for g in range(2):
-                raw = tile([P, 4, width], F32, f"{name}{g}")
-                nc.sync.dma_start(
-                    raw[:], w1[512 * g : 512 * (g + 1), c0 : c0 + width].rearrange("(p j) c -> p j c", j=4)
-                )
+                raw = tile([P, 4, width], F32, f"{name}{g}", late)
+                rows = w1[K_PASS * g : K_PASS * (g + 1), c0 : c0 + width]
+                nc.sync.dma_start(raw[:], rows.rearrange("(p s) c -> p s c", s=4))
                 raws.append(raw)
             return raws
 
-        raw0 = load_w1(0, P, "raw0_")
-        xw = []
-        for g in range(2):
-            words = tile([P, T], I32, f"xw{g}")
-            nc.sync.dma_start(words[:], x_words[g].rearrange("p n t -> p (n t)").bitcast(I32))
-            xw.append(words)
-        raw1 = load_w1(P, P, "raw1_")
-        rawb = load_w1(2 * P, 2 * P, "rawb_")
-        skip_sb = []
-        w2_raw = tile([P, 2, 4, N], F32, "w2_raw")
-        for t in range(4):
-            if t == 3:
-                for half in range(2):
-                    nc.sync.dma_start(
-                        w2_raw[64 * half : 64 * (half + 1)].rearrange("p a s n -> p a (s n)"),
-                        w2.rearrange("(a p s) n -> p a (s n)", a=2, s=4),
-                    )
-            rows = tile([P, U], F32, f"skip{t}")
-            if t < 2:
-                nc.sync.dma_start(rows[:], skip[P * t : P * (t + 1), :])
-            else:
-                nc.sync.dma_start(
-                    rows[:], skip[2 * P :, :].rearrange("(q u e) v -> u q e v", u=2, e=2)[t - 2]
-                )
-            skip_sb.append(rows)
+        def load_skip(t, rows):
+            skip_tile = tile([P, U], F32, f"skip{t}", late)
+            nc.sync.dma_start(skip_tile[:], rows)
+            return skip_tile
 
-        ident = tile([P, P], F32, "ident")
-        make_identity(nc, ident[:])
+        w1_raw0 = load_w1(0, P, "w1_raw0_")
+        x_words_sb.append(load_words(1, late))
+        w1_raw1 = load_w1(P, P, "w1_raw1_")
+        w1_raw23 = load_w1(2 * P, 2 * P, "w1_raw23_")
+        w2_raw = tile([P, 2, 4, N], F32, "w2_raw", late)
+        skip_pairs = skip[2 * P :, :].rearrange("(r u e) v -> u r e v", u=2, e=2)
+        skip_sb = [load_skip(0, skip[:P, :]), load_skip(1, skip[P : 2 * P, :]), load_skip(2, skip_pairs[0])]
+        for half in range(2):
+            nc.sync.dma_start(
+                w2_raw[HALF_P * half : HALF_P * (half + 1)].rearrange("p a s m -> p a (s m)"),
+                w2.rearrange("(a p s) m -> p a (s m)", a=2, s=4),
+            )
+        skip_sb.append(load_skip(3, skip_pairs[1]))
 
-        up = []
-        for t in range(4):
-            window = tile([P, U], F32, f"up{t}")
-            nc.vector.memset(window[:], 0.0)
-            up.append(window)
+        up = [tile([P, U], F32, f"up{t}") for t in range(3)]
+        nc.vector.memset(up[0][:], 0.0)
+        nc.scalar.copy(up[1][:], up[0][:])
+        nc.vector.memset(up[2][:], 0.0)
+        up.append(up[0])
         w2_codes = tile([P, 2, 2 * N], U32, "w2_codes")
         nc.vector.memset(w2_codes[:].bitcast(I32), 0)
 
@@ -102,32 +119,30 @@ def tile_picked_unet_gelu_p_kernel(
             nc.vector.quantize_mx(out=codes[:].bitcast(FP8X4), scales=scales[:], in_=src)
             return codes, scales
 
-        def cast_w1(raws, name):
+        def quantize_w1_tile(raws, name):
             grouped = tile([P, 2, P, 4], BF16, name)
             for g in range(2):
                 nc.scalar.copy(
-                    grouped[:, g].rearrange("p (c i) j -> p c j i", i=4),
-                    raws[g][:].rearrange("p j (c i) -> p c j i", i=4),
+                    grouped[:, g].rearrange("p (c n) s -> p c s n", n=4),
+                    raws[g][:].rearrange("p s (c n) -> p c s n", n=4),
                 )
-            return quantize(grouped[:].rearrange("p g c j -> p (g c j)"), name)
+            return quantize(grouped[:].rearrange("p g c s -> p (g c s)"), name)
 
-        wq0 = cast_w1(raw0, "wb0")
+        w1_q0 = quantize_w1_tile(w1_raw0, "w1_bf0")
 
-        xg_scales = tile([P, S], U8, "xg_scales")
-        nc.vector.tensor_copy(xg_scales[:], xs[:].indirect(offs_sb[:]))
-        xg0 = tile([P, S], U32, "xg0")
-        nc.vector.tensor_copy(xg0[:], xw[0][:].bitcast(U32).indirect(offs_sb[:]))
-        xg1 = tile([P, S], U32, "xg1")
-        for part in range(2):
+        picked_scales = tile([P, S], U8, "picked_scales")
+        nc.vector.tensor_copy(picked_scales[:], x_scales_sb[:].indirect(offs_sb[:]))
+        picked_words = [tile([P, S], U32, f"picked_words{g}") for g in range(2)]
+        nc.vector.tensor_copy(picked_words[0][:], x_words_sb[0][:].bitcast(U32).indirect(offs_sb[:]))
+        for lo in (0, HALF_S):
             nc.vector.tensor_copy(
-                xg1[:, HALF_S * part : HALF_S * (part + 1)],
-                xw[1][:].bitcast(U32).indirect(offs_sb[:, HALF_COLS * part : HALF_COLS * (part + 1)]),
+                picked_words[1][:, lo : lo + HALF_S],
+                x_words_sb[1][:].bitcast(U32).indirect(entries(offs_sb, lo, lo + HALF_S)),
             )
-        xg = [xg0, xg1]
 
-        def first_product(bank, wq, col0, *bounds):
-            codes, scales = wq
-            acc = ps.tile([P, bounds[-1] - bounds[0]], F32, name=f"back{bank}", tag=f"back{bank}")
+        def first_product(tag, w1_q, col0, *bounds):
+            codes, scales = w1_q
+            acc = psum([P, bounds[-1] - bounds[0]], tag)
             for lo, hi in zip(bounds, bounds[1:]):
                 for g in range(2):
                     cols = slice(col0 + P * g, col0 + P * (g + 1))
@@ -135,125 +150,135 @@ def tile_picked_unet_gelu_p_kernel(
                         acc[:, lo - bounds[0] : hi - bounds[0]],
                         lhsT=codes[:, cols].bitcast(FP8X4),
                         lhsT_scale=scales[:, cols],
-                        rhs=xg[g][:, lo:hi].bitcast(FP8X4),
-                        rhs_scale=xg_scales[4 * g :, lo:hi],
+                        rhs=picked_words[g][:, lo:hi].bitcast(FP8X4),
+                        rhs_scale=picked_scales[4 * g :, lo:hi],
                         start=(g == 0),
                         stop=(g == 1),
                     )
             return acc
 
-        def gelu_scatter(t, acc, h_sb, offsets):
-            nc.scalar.activation(h_sb, acc, GELU)
-            nc.vector.tensor_copy(up[t][:].indirect(offsets), h_sb)
+        def scatter(t, h_sb, lo, hi):
+            nc.vector.tensor_copy(up[t][:].indirect(entries(cell_sb, lo, hi)), h_sb)
 
-        cell_first, cell_second = cell_sb[:, :HALF_COLS], cell_sb[:, HALF_COLS:]
+        def gelu_scatter(t, acc, h_sb, lo, hi):
+            nc.scalar.activation(h_sb, acc[:], GELU)
+            scatter(t, h_sb, lo, hi)
 
-        acc0a = first_product(0, wq0, 0, 0, HALF_S)
-        acc0b = first_product(1, wq0, 0, HALF_S, S)
-        h0a = tile([P, HALF_S], F32, "h0a")
-        gelu_scatter(0, acc0a[:], h0a[:], cell_first)
-        wq1 = cast_w1(raw1, "wb1")
-        gelu_scatter(0, acc0b[:], raw1[1][:].rearrange("p j c -> p (j c)")[:, :HALF_S], cell_second)
+        def spent(raw, width):
+            return raw[:].rearrange("p s c -> p (s c)")[:, :width]
 
-        acc1a = first_product(2, wq1, 0, 0, P)
-        acc1b = first_product(3, wq1, 0, P, 2 * P, S)
-        h1a = tile([P, P], F32, "h1a")
-        gelu_scatter(1, acc1a[:], h1a[:], cell_sb[:, : P // 16])
-        wbb = tile([P, 2, 2, P, 4], BF16, "wbb")
+        acc0_first = first_product("back0", w1_q0, 0, 0, HALF_S)
+        acc0_second = first_product("back1", w1_q0, 0, HALF_S, S)
+        h0_first = tile([P, HALF_S], F32, "h0_first")
+        gelu_scatter(0, acc0_first, h0_first[:], 0, HALF_S)
+        w1_q1 = quantize_w1_tile(w1_raw1, "w1_bf1")
+        gelu_scatter(0, acc0_second, spent(w1_raw1[1], HALF_S), HALF_S, S)
+
+        acc1_head = first_product("back2", w1_q1, 0, 0, HEAD_S)
+        acc1_rest = first_product("back3", w1_q1, 0, HEAD_S, HALF_S, S)
+        h1_head = tile([P, HEAD_S], F32, "h1_head")
+        gelu_scatter(1, acc1_head, h1_head[:], 0, HEAD_S)
+        w1_bf23 = tile([P, 2, 2, P, 4], BF16, "w1_bf23")
         for g in range(2):
             nc.scalar.copy(
-                wbb[:, :, g].rearrange("p u (q e) j -> p u q j e", e=2),
-                rawb[g][:].rearrange("p j (q u e) -> p u q j e", u=2, e=2),
+                w1_bf23[:, :, g].rearrange("p u (r e) s -> p u r s e", e=2),
+                w1_raw23[g][:].rearrange("p s (r u e) -> p u r s e", u=2, e=2),
             )
-        wqb = quantize(wbb[:].rearrange("p u g c j -> p (u g c j)"), "wbb")
-        gelu_scatter(1, acc1b[:], rawb[1][:].rearrange("p j c -> p (j c)")[:, : S - P], cell_sb[:, P // 16 :])
+        w1_q23 = quantize(w1_bf23[:].rearrange("p u g c s -> p (u g c s)"), "w1_bf23")
+        gelu_scatter(1, acc1_rest, spent(w1_raw23[1], S - HEAD_S), HEAD_S, S)
 
+        h23 = []
         for u in range(2):
-            acc = first_product(u, wqb, 2 * P * u, 0, S)
+            acc = first_product(f"back{u}", w1_q23, 2 * P * u, 0, S)
             h_sb = tile([P, S], F32, f"h{2 + u}")
-            gelu_scatter(2 + u, acc[:], h_sb[:], cell_sb[:])
+            nc.scalar.activation(h_sb[:], acc[:], GELU)
+            h23.append(h_sb)
+        scatter(2, h23[0][:], 0, S)
 
         def turn_and_add(t, tags):
-            pairs = 4 // len(tags)
-            banks = [ps.tile([P, pairs, 2, P], F32, name=tag, tag=tag) for tag in tags]
+            per_bank = STRIPES // len(tags)
+            banks = [psum([P, per_bank, 2, P], tag) for tag in tags]
             for src in (skip_sb[t], up[t]):
-                for j in range(4):
+                for j in range(STRIPES):
                     for half in range(2):
-                        v0 = 512 * half + P * j
+                        v0 = HALF_U * half + P * j
                         nc.tensor.matmul(
-                            banks[j // pairs][:, j % pairs, half, :],
+                            banks[j // per_bank][:, j % per_bank, half, :],
                             lhsT=src[:, v0 : v0 + P],
                             rhs=ident[:],
                             is_transpose=True,
-                            start=(src is skip_sb[t] and j % pairs == 0 and half == 0),
-                            stop=(src is up[t] and j % pairs == pairs - 1 and half == 1),
+                            start=(src is skip_sb[t] and j % per_bank == 0 and half == 0),
+                            stop=(src is up[t] and j % per_bank == per_bank - 1 and half == 1),
                         )
             return banks
 
-        zt_a = [tile([P, 2, 4, P], BF16, f"zt_a{jj}") for jj in range(2)]
+        z0_turned = [tile([P, 2, 4, P], BF16, f"z0_turned{jj}") for jj in range(2)]
         for t in range(2):
             for jj, bank in enumerate(turn_and_add(t, (f"turned{2 * t}", f"turned{2 * t + 1}"))):
                 nc.scalar.copy(
-                    zt_a[jj][:, :, :, 64 * t : 64 * (t + 1)].rearrange("p u b (q e) -> p b u q e", e=2),
-                    bank[:].rearrange("p j h (q u e) -> p (j h) u q e", u=2, e=2),
+                    z0_turned[jj][:, :, :, HALF_P * t : HALF_P * (t + 1)].rearrange("p u b (r e) -> p b u r e", e=2),
+                    bank[:].rearrange("p j h (r u e) -> p (j h) u r e", u=2, e=2),
                 )
-        zq_a = tile([P, 2 * U], BF16, "zq_a")
+        scatter(3, h23[1][:], 0, S)
+        z0_bf = tile([P, 4 * HALF_U], BF16, "z0_bf")
         for jj in range(2):
-            back = ps.tile([P, 2, 2, P], F32, name=f"back{jj}", tag=f"back{jj}")
+            back = psum([P, 2, 2, P], f"back{jj}")
             for j in range(2):
                 for u in range(2):
-                    words = zt_a[jj][:, u, 2 * j : 2 * j + 2, :].rearrange("p h c -> p (h c)").bitcast(F32)
+                    words = z0_turned[jj][:, u, 2 * j : 2 * j + 2, :].rearrange("p h m -> p (h m)").bitcast(F32)
                     nc.tensor.transpose(back[:, j, u, :], words, ident[:])
             nc.scalar.copy(
-                zq_a[:, U * jj : U * (jj + 1)].bitcast(F32).rearrange("p (j v u) -> p j v u", j=2, u=2),
-                back[:].rearrange("p j u v -> p j v u"),
+                z0_bf[:, 8 * P * jj : 8 * P * (jj + 1)].bitcast(F32).rearrange("p (j c u) -> p j c u", j=2, u=2),
+                back[:].rearrange("p j u c -> p j c u"),
             )
 
         w2_bf = tile([P, 2, N, 4], BF16, "w2_bf")
         nc.scalar.copy(
-            w2_bf[:].rearrange("p a (c i) s -> p a c s i", i=4),
-            w2_raw[:].rearrange("p a s (c i) -> p a c s i", i=4),
+            w2_bf[:].rearrange("p a (c n) s -> p a c s n", n=4),
+            w2_raw[:].rearrange("p a s (c n) -> p a c s n", n=4),
         )
 
-        zt_low = [tile([P, 2, 2 * P], BF16, f"zt_low{jj}") for jj in range(2)]
+        z1_pair0 = [tile([P, 2, 2 * P], BF16, f"z1_pair0_{jj}") for jj in range(2)]
         for jj, bank in enumerate(turn_and_add(2, ("back2", "back3"))):
-            nc.scalar.copy(zt_low[jj][:], bank[:].rearrange("p j h c -> p j (h c)"))
-        backs = [ps.tile([P, 2, P], F32, name=f"back{j}", tag=f"back{j}") for j in range(4)]
-        for j in range(4):
-            nc.tensor.transpose(backs[j][:, 0, :], zt_low[j // 2][:, j % 2, :].bitcast(F32), ident[:])
-        for j, bank in enumerate(turn_and_add(3, [f"turned{j}" for j in range(4)])):
-            zt_high = tile([P, 2 * P], BF16, f"zt_high{j}")
-            copy = nc.vector.tensor_copy if j == 3 else nc.scalar.copy
-            copy(zt_high[:], bank[:].rearrange("p j h c -> p (j h c)"))
-            nc.tensor.transpose(backs[j][:, 1, :], zt_high[:].bitcast(F32), ident[:])
+            nc.scalar.copy(z1_pair0[jj][:], bank[:].rearrange("p j h m -> p j (h m)"))
+        backs = [psum([P, 2, P], f"back{j}") for j in range(STRIPES)]
+        for j in range(STRIPES):
+            nc.tensor.transpose(backs[j][:, 0, :], z1_pair0[j // 2][:, j % 2, :].bitcast(F32), ident[:])
+        for j, bank in enumerate(turn_and_add(3, [f"turned{j}" for j in range(STRIPES)])):
+            z1_pair1 = tile([P, 2 * P], BF16, f"z1_pair1_{j}")
+            copy = nc.vector.tensor_copy if j == STRIPES - 1 else nc.scalar.copy
+            copy(z1_pair1[:], bank[:].rearrange("p j h m -> p (j h m)"))
+            nc.tensor.transpose(backs[j][:, 1, :], z1_pair1[:].bitcast(F32), ident[:])
 
-        w2_both, w2_scales = quantize(w2_bf[:].rearrange("p a n s -> p (a n s)"), "w2q")
+        w2_both, w2_scales = quantize(w2_bf[:].rearrange("p a m s -> p (a m s)"), "w2_both")
         for half in range(2):
-            rows = slice(64 * half, 64 * (half + 1))
+            rows = slice(HALF_P * half, HALF_P * (half + 1))
             nc.vector.tensor_copy(w2_codes[rows, half, :], w2_both[rows, :])
-        za = quantize(zq_a[:], "za")
+        z0_codes, z0_scales = quantize(z0_bf[:], "z0")
 
-        out_view = out.rearrange("m (h j c) -> m j h c", h=2, j=4)
-        for j in range(4):
-            zq_b = tile([P, 4 * P], BF16, f"zq_b{j}")
+        out_stripes = out.rearrange("m (h j c) -> m j h c", h=2, j=STRIPES)
+        for j in range(STRIPES):
+            z1_bf = tile([P, 4 * P], BF16, f"z1_bf{j}")
             nc.scalar.copy(
-                zq_b[:].bitcast(F32).rearrange("p (v u) -> p v u", u=2), backs[j][:].rearrange("p u v -> p v u")
+                z1_bf[:].bitcast(F32).rearrange("p (c u) -> p c u", u=2), backs[j][:].rearrange("p u c -> p c u")
             )
-            zb = quantize(zq_b[:], f"zb{j}")
-            acc = ps.tile([P, 2, P], F32, name=f"turned{j}", tag=f"turned{j}")
-            for a, (codes, scales, cols) in enumerate((za + (slice(P * j, P * (j + 1)),), zb + (slice(0, P),))):
+            z1_codes, z1_scales = quantize(z1_bf[:], f"z1_{j}")
+            stripe = slice(P * j, P * (j + 1))
+            moving = ((z0_codes[:, stripe], z0_scales[:, stripe]), (z1_codes[:], z1_scales[:]))
+            acc = psum([P, 2, P], f"turned{j}")
+            for a, (codes, scales) in enumerate(moving):
                 w_cols = slice(N * a, N * (a + 1))
                 for half in range(2):
                     nc.tensor.matmul_mx(
                         acc[:, half, :],
                         lhsT=w2_codes[:, half, w_cols].bitcast(FP8X4),
                         lhsT_scale=w2_scales[:, w_cols],
-                        rhs=codes[:, cols].bitcast(FP8X4),
-                        rhs_scale=scales[:, cols],
+                        rhs=codes.bitcast(FP8X4),
+                        rhs_scale=scales,
                         start=(a == 0 and half == 0),
                         stop=(a == 1 and half == 1),
                     )
             result = tile([P, 2, P], F32, f"result{j}")
             copy = nc.scalar.copy if j % 2 == 0 else nc.vector.tensor_copy
             copy(result[:], acc[:])
-            nc.sync.dma_start(out_view[:, j], result[:])
+            nc.sync.dma_start(out_stripes[:, j], result[:])

@@ -13,15 +13,15 @@ U16 = mybir.dt.uint16
 U8 = mybir.dt.uint8
 FP8X4 = mybir.dt.float8_e4m3fn_x4
 GELU = mybir.ActivationFunctionType.Gelu_apprx_tanh
+COPY = mybir.ActivationFunctionType.Copy
+ADD = mybir.AluOpType.add
 
 P = 128
-HALF_P = P // 2
 K_PASS = 4 * P
-HALF_U = U // 2
-STRIPES = HALF_U // P
 LIST_ROWS = 16
-HALF_S = S // 2
-HEAD_S = 128
+HEAD_S = 256
+CHUNK = 256
+CAST_V = 80
 
 
 def tile_picked_unet_gelu_p_kernel(
@@ -32,8 +32,8 @@ def tile_picked_unet_gelu_p_kernel(
         sb = ctx.enter_context(tc.tile_pool(name="sb", bufs=1))
         ps = ctx.enter_context(tc.psum_pool(name="ps", bufs=1))
 
-        def tile(shape, dtype, name, pool=sb):
-            return pool.tile(shape, dtype, name=name, align_bytes=64)
+        def tile(shape, dtype, name, tag=None):
+            return sb.tile(shape, dtype, name=name, tag=tag or name, align_bytes=64)
 
         def psum(shape, tag):
             return ps.tile(shape, F32, name=tag, tag=tag)
@@ -46,71 +46,28 @@ def tile_picked_unet_gelu_p_kernel(
         nc.sync.dma_start(offs_sb[:], offs)
         nc.sync.dma_start(cell_sb[:], cell)
 
-        def load_words(g, pool):
-            words = tile([P, T], I32, f"x_words{g}", pool)
-            nc.sync.dma_start(words[:], x_words[g].rearrange("p n s -> p (n s)").bitcast(I32))
-            return words
-
-        x_words_sb = [load_words(0, sb)]
-
-        x_scales_sb = tile([P, T], U8, "x_scales_sb")
-        nc.vector.memset(x_scales_sb[:].bitcast(I32), 0)
+        x_scales_sb = tile([P, T], U8, "x_scales_sb", "chain")
+        nc.gpsimd.memset(x_scales_sb[:].bitcast(I32), 0)
         for q in range(4):
             nc.sync.dma_start(
                 x_scales_sb[32 * q : 32 * q + 8, :].bitcast(I32),
                 x_scales[:, 4 * q : 4 * q + 4, :].bitcast(I32),
             )
 
-        ident = tile([P, P], F32, "ident")
-        with tc.tile_pool(name="early", bufs=1) as early:
-            ones = tile([P, P], F32, "ones", early)
-            nc.gpsimd.memset(ones[:], 1.0)
-            nc.gpsimd.affine_select(
-                out=ident[:],
-                in_=ones[:],
-                compare_op=mybir.AluOpType.is_equal,
-                fill=0.0,
-                base=0,
-                pattern=[[-1, P]],
-                channel_multiplier=1,
-            )
-        late = ctx.enter_context(tc.tile_pool(name="late", bufs=1))
+        w1_raw, x_words_sb = [], []
+        for g in range(2):
+            raw = tile([P, 4, H], F32, f"w1_raw{g}", f"raw{g}")
+            nc.sync.dma_start(raw[:], w1[K_PASS * g : K_PASS * (g + 1), :].rearrange("(p s) c -> p s c", s=4))
+            w1_raw.append(raw)
+            words = tile([P, T], I32, f"x_words{g}")
+            nc.sync.dma_start(words[:], x_words[g].rearrange("p n s -> p (n s)").bitcast(I32))
+            x_words_sb.append(words)
 
-        def load_w1(c0, width, name):
-            raws = []
-            for g in range(2):
-                raw = tile([P, 4, width], F32, f"{name}{g}", late)
-                rows = w1[K_PASS * g : K_PASS * (g + 1), c0 : c0 + width]
-                nc.sync.dma_start(raw[:], rows.rearrange("(p s) c -> p s c", s=4))
-                raws.append(raw)
-            return raws
-
-        def load_skip(t, rows):
-            skip_tile = tile([P, U], F32, f"skip{t}", late)
-            nc.sync.dma_start(skip_tile[:], rows)
-            return skip_tile
-
-        w1_raw0 = load_w1(0, P, "w1_raw0_")
-        x_words_sb.append(load_words(1, late))
-        w1_raw1 = load_w1(P, P, "w1_raw1_")
-        w1_raw23 = load_w1(2 * P, 2 * P, "w1_raw23_")
-        w2_raw = tile([P, 2, 4, N], F32, "w2_raw", late)
-        skip_pairs = skip[2 * P :, :].rearrange("(r u e) v -> u r e v", u=2, e=2)
-        skip_sb = [load_skip(0, skip[:P, :]), load_skip(1, skip[P : 2 * P, :]), load_skip(2, skip_pairs[0])]
-        for half in range(2):
-            nc.sync.dma_start(
-                w2_raw[HALF_P * half : HALF_P * (half + 1)].rearrange("p a s m -> p a (s m)"),
-                w2.rearrange("(a p s) m -> p a (s m)", a=2, s=4),
-            )
-        skip_sb.append(load_skip(3, skip_pairs[1]))
-
-        up = [tile([P, U], F32, f"up{t}") for t in range(3)]
+        up = [tile([P, U], F32, f"up{t}") for t in range(4)]
         nc.vector.memset(up[0][:], 0.0)
-        nc.scalar.copy(up[1][:], up[0][:])
-        nc.vector.memset(up[2][:], 0.0)
-        up.append(up[0])
-        w2_codes = tile([P, 2, 2 * N], U32, "w2_codes")
-        nc.vector.memset(w2_codes[:].bitcast(I32), 0)
+        nc.scalar.copy(up[2][:], up[0][:])
+        nc.vector.memset(up[1][:], 0.0)
+        nc.vector.memset(up[3][:], 0.0)
 
         def quantize(src, name):
             width = src.shape[1] // 4
@@ -119,166 +76,103 @@ def tile_picked_unet_gelu_p_kernel(
             nc.vector.quantize_mx(out=codes[:].bitcast(FP8X4), scales=scales[:], in_=src)
             return codes, scales
 
-        def quantize_w1_tile(raws, name):
-            grouped = tile([P, 2, P, 4], BF16, name)
-            for g in range(2):
-                nc.scalar.copy(
-                    grouped[:, g].rearrange("p (c n) s -> p c s n", n=4),
-                    raws[g][:].rearrange("p s (c n) -> p c s n", n=4),
-                )
-            return quantize(grouped[:].rearrange("p g c s -> p (g c s)"), name)
-
-        w1_q0 = quantize_w1_tile(w1_raw0, "w1_bf0")
+        def cast_w1(copy, grouped, raw, m0, m1):
+            copy(
+                grouped[:, :, m0:m1, :].rearrange("p t m s -> p m s t"),
+                raw[:].rearrange("p s (m t) -> p m s t", t=4)[:, m0:m1],
+            )
 
         picked_scales = tile([P, S], U8, "picked_scales")
         nc.vector.tensor_copy(picked_scales[:], x_scales_sb[:].indirect(offs_sb[:]))
-        picked_words = [tile([P, S], U32, f"picked_words{g}") for g in range(2)]
+        w1_bf0 = tile([P, 4, P, 4], BF16, "w1_bf0", "bf0")
+        cast_w1(nc.vector.tensor_copy, w1_bf0, w1_raw[0], 0, P)
+        w1_q = [quantize(w1_bf0[:].rearrange("p t m s -> p (t m s)"), "w1_q0")]
+        picked_words = [tile([P, S], U32, "picked_words0")]
         nc.vector.tensor_copy(picked_words[0][:], x_words_sb[0][:].bitcast(U32).indirect(offs_sb[:]))
-        for lo in (0, HALF_S):
+        w1_bf1 = tile([P, 4, P, 4], BF16, "w1_bf1", "chain")
+        cast_w1(nc.vector.tensor_copy, w1_bf1, w1_raw[1], 0, CAST_V)
+        cast_w1(nc.scalar.copy, w1_bf1, w1_raw[1], CAST_V, P)
+        w1_q.append(quantize(w1_bf1[:].rearrange("p t m s -> p (t m s)"), "w1_q1"))
+        picked_words.append(tile([P, S], U32, "picked_words1", "chain"))
+        for lo, hi in ((0, HEAD_S), (HEAD_S, S)):
             nc.vector.tensor_copy(
-                picked_words[1][:, lo : lo + HALF_S],
-                x_words_sb[1][:].bitcast(U32).indirect(entries(offs_sb, lo, lo + HALF_S)),
+                picked_words[1][:, lo:hi], x_words_sb[1][:].bitcast(U32).indirect(entries(offs_sb, lo, hi))
             )
 
-        def first_product(tag, w1_q, col0, *bounds):
-            codes, scales = w1_q
-            acc = psum([P, bounds[-1] - bounds[0]], tag)
-            for lo, hi in zip(bounds, bounds[1:]):
-                for g in range(2):
-                    cols = slice(col0 + P * g, col0 + P * (g + 1))
+        skip_rows = skip.rearrange("(p t) v -> p t v", t=4)
+        skip_sb = []
+        for u in range(2):
+            pair = tile([P, 2, U], F32, f"skip{u}", f"raw{u}")
+            nc.sync.dma_start(pair[:], skip_rows[:, 2 * u : 2 * u + 2, :])
+            skip_sb.append(pair)
+        w2_raw = tile([P, 4, N], F32, "w2_raw", "bf0")
+        nc.sync.dma_start(w2_raw[:], w2.rearrange("(p s) m -> p s m", s=4))
+
+        pieces = [(0, (0, HEAD_S)), (0, (HEAD_S, S))] + [(t, (0, S)) for t in range(1, 4)]
+        banks = [psum([P, b[-1] - b[0]], f"bank{n}") for n, (t, b) in enumerate(pieces)]
+        for g in range(2):
+            codes, scales = w1_q[g]
+            for bank, (t, bounds) in zip(banks, pieces):
+                cols = slice(P * t, P * (t + 1))
+                for lo, hi in zip(bounds, bounds[1:]):
                     nc.tensor.matmul_mx(
-                        acc[:, lo - bounds[0] : hi - bounds[0]],
+                        bank[:, lo - bounds[0] : hi - bounds[0]],
                         lhsT=codes[:, cols].bitcast(FP8X4),
                         lhsT_scale=scales[:, cols],
                         rhs=picked_words[g][:, lo:hi].bitcast(FP8X4),
                         rhs_scale=picked_scales[4 * g :, lo:hi],
-                        start=(g == 0),
-                        stop=(g == 1),
+                        start=(g == 0 and lo == bounds[0]),
+                        stop=(g == 1 and hi == bounds[-1]),
                     )
-            return acc
+        h = []
+        for n, (bank, (t, bounds)) in enumerate(zip(banks, pieces)):
+            h_sb = tile([P, bounds[-1] - bounds[0]], F32, f"h{n}")
+            nc.scalar.activation(h_sb[:], bank[:], GELU)
+            h.append(h_sb)
+        for h_sb, (t, bounds) in zip(h, pieces):
+            if t < 2:
+                nc.vector.tensor_copy(up[t][:].indirect(entries(cell_sb, bounds[0], bounds[-1])), h_sb[:])
+            else:
+                for lo in (0, S // 2):
+                    hi = lo + S // 2
+                    nc.scalar.activation(up[t][:].indirect(entries(cell_sb, lo, hi)), h_sb[:, lo:hi], COPY)
 
-        def scatter(t, h_sb, lo, hi):
-            nc.vector.tensor_copy(up[t][:].indirect(entries(cell_sb, lo, hi)), h_sb)
+        chunks = range(U // CHUNK)
+        planes = [tile([P, 4, CHUNK], BF16, f"planes{c}") for c in chunks]
 
-        def gelu_scatter(t, acc, h_sb, lo, hi):
-            nc.scalar.activation(h_sb, acc[:], GELU)
-            scatter(t, h_sb, lo, hi)
+        def add_skip(t, c):
+            cells = slice(CHUNK * c, CHUNK * (c + 1))
+            nc.vector.tensor_tensor(planes[c][:, t, :], up[t][:, cells], skip_sb[t // 2][:, t % 2, cells], ADD)
 
-        def spent(raw, width):
-            return raw[:].rearrange("p s c -> p (s c)")[:, :width]
-
-        acc0_first = first_product("back0", w1_q0, 0, 0, HALF_S)
-        acc0_second = first_product("back1", w1_q0, 0, HALF_S, S)
-        h0_first = tile([P, HALF_S], F32, "h0_first")
-        gelu_scatter(0, acc0_first, h0_first[:], 0, HALF_S)
-        w1_q1 = quantize_w1_tile(w1_raw1, "w1_bf1")
-        gelu_scatter(0, acc0_second, spent(w1_raw1[1], HALF_S), HALF_S, S)
-
-        acc1_head = first_product("back2", w1_q1, 0, 0, HEAD_S)
-        acc1_rest = first_product("back3", w1_q1, 0, HEAD_S, HALF_S, S)
-        h1_head = tile([P, HEAD_S], F32, "h1_head")
-        gelu_scatter(1, acc1_head, h1_head[:], 0, HEAD_S)
-        w1_bf23 = tile([P, 2, 2, P, 4], BF16, "w1_bf23")
-        for g in range(2):
-            nc.scalar.copy(
-                w1_bf23[:, :, g].rearrange("p u (r e) s -> p u r s e", e=2),
-                w1_raw23[g][:].rearrange("p s (r u e) -> p u r s e", u=2, e=2),
-            )
-        w1_q23 = quantize(w1_bf23[:].rearrange("p u g c s -> p (u g c s)"), "w1_bf23")
-        gelu_scatter(1, acc1_rest, spent(w1_raw23[1], S - HEAD_S), HEAD_S, S)
-
-        h23 = []
-        for u in range(2):
-            acc = first_product(f"back{u}", w1_q23, 2 * P * u, 0, S)
-            h_sb = tile([P, S], F32, f"h{2 + u}")
-            nc.scalar.activation(h_sb[:], acc[:], GELU)
-            h23.append(h_sb)
-        scatter(2, h23[0][:], 0, S)
-
-        def turn_and_add(t, tags):
-            per_bank = STRIPES // len(tags)
-            banks = [psum([P, per_bank, 2, P], tag) for tag in tags]
-            for src in (skip_sb[t], up[t]):
-                for j in range(STRIPES):
-                    for half in range(2):
-                        v0 = HALF_U * half + P * j
-                        nc.tensor.matmul(
-                            banks[j // per_bank][:, j % per_bank, half, :],
-                            lhsT=src[:, v0 : v0 + P],
-                            rhs=ident[:],
-                            is_transpose=True,
-                            start=(src is skip_sb[t] and j % per_bank == 0 and half == 0),
-                            stop=(src is up[t] and j % per_bank == per_bank - 1 and half == 1),
-                        )
-            return banks
-
-        z0_turned = [tile([P, 2, 4, P], BF16, f"z0_turned{jj}") for jj in range(2)]
         for t in range(2):
-            for jj, bank in enumerate(turn_and_add(t, (f"turned{2 * t}", f"turned{2 * t + 1}"))):
-                nc.scalar.copy(
-                    z0_turned[jj][:, :, :, HALF_P * t : HALF_P * (t + 1)].rearrange("p u b (r e) -> p b u r e", e=2),
-                    bank[:].rearrange("p j h (r u e) -> p (j h) u r e", u=2, e=2),
-                )
-        scatter(3, h23[1][:], 0, S)
-        z0_bf = tile([P, 4 * HALF_U], BF16, "z0_bf")
-        for jj in range(2):
-            back = psum([P, 2, 2, P], f"back{jj}")
-            for j in range(2):
-                for u in range(2):
-                    words = z0_turned[jj][:, u, 2 * j : 2 * j + 2, :].rearrange("p h m -> p (h m)").bitcast(F32)
-                    nc.tensor.transpose(back[:, j, u, :], words, ident[:])
-            nc.scalar.copy(
-                z0_bf[:, 8 * P * jj : 8 * P * (jj + 1)].bitcast(F32).rearrange("p (j c u) -> p j c u", j=2, u=2),
-                back[:].rearrange("p j u c -> p j c u"),
-            )
-
-        w2_bf = tile([P, 2, N, 4], BF16, "w2_bf")
-        nc.scalar.copy(
-            w2_bf[:].rearrange("p a (c n) s -> p a c s n", n=4),
-            w2_raw[:].rearrange("p a s (c n) -> p a c s n", n=4),
+            for c in chunks:
+                add_skip(t, c)
+        w2_bf = tile([P, N, 4], BF16, "w2_bf")
+        nc.vector.tensor_copy(
+            w2_bf[:].rearrange("p (c n) s -> p c s n", n=4), w2_raw[:].rearrange("p s (c n) -> p c s n", n=4)
         )
+        for c in chunks:
+            add_skip(2, c)
+            add_skip(3, c)
+        w2_codes, w2_scales = quantize(w2_bf[:].rearrange("p m s -> p (m s)"), "w2")
 
-        z1_pair0 = [tile([P, 2, 2 * P], BF16, f"z1_pair0_{jj}") for jj in range(2)]
-        for jj, bank in enumerate(turn_and_add(2, ("back2", "back3"))):
-            nc.scalar.copy(z1_pair0[jj][:], bank[:].rearrange("p j h m -> p j (h m)"))
-        backs = [psum([P, 2, P], f"back{j}") for j in range(STRIPES)]
-        for j in range(STRIPES):
-            nc.tensor.transpose(backs[j][:, 0, :], z1_pair0[j // 2][:, j % 2, :].bitcast(F32), ident[:])
-        for j, bank in enumerate(turn_and_add(3, [f"turned{j}" for j in range(STRIPES)])):
-            z1_pair1 = tile([P, 2 * P], BF16, f"z1_pair1_{j}")
-            copy = nc.vector.tensor_copy if j == STRIPES - 1 else nc.scalar.copy
-            copy(z1_pair1[:], bank[:].rearrange("p j h m -> p (j h m)"))
-            nc.tensor.transpose(backs[j][:, 1, :], z1_pair1[:].bitcast(F32), ident[:])
-
-        w2_both, w2_scales = quantize(w2_bf[:].rearrange("p a m s -> p (a m s)"), "w2_both")
-        for half in range(2):
-            rows = slice(HALF_P * half, HALF_P * (half + 1))
-            nc.vector.tensor_copy(w2_codes[rows, half, :], w2_both[rows, :])
-        z0_codes, z0_scales = quantize(z0_bf[:], "z0")
-
-        out_stripes = out.rearrange("m (h j c) -> m j h c", h=2, j=STRIPES)
-        for j in range(STRIPES):
-            z1_bf = tile([P, 4 * P], BF16, f"z1_bf{j}")
-            nc.scalar.copy(
-                z1_bf[:].bitcast(F32).rearrange("p (c u) -> p c u", u=2), backs[j][:].rearrange("p u c -> p c u")
+        for c in chunks:
+            z_bf = tile([P, CHUNK, 4], BF16, f"z_bf{c}")
+            copy = nc.scalar.copy if c < 2 else nc.vector.tensor_copy
+            copy(
+                z_bf[:].rearrange("p (c n) t -> p c t n", n=4), planes[c][:].rearrange("p t (c n) -> p c t n", n=4)
             )
-            z1_codes, z1_scales = quantize(z1_bf[:], f"z1_{j}")
-            stripe = slice(P * j, P * (j + 1))
-            moving = ((z0_codes[:, stripe], z0_scales[:, stripe]), (z1_codes[:], z1_scales[:]))
-            acc = psum([P, 2, P], f"turned{j}")
-            for a, (codes, scales) in enumerate(moving):
-                w_cols = slice(N * a, N * (a + 1))
-                for half in range(2):
-                    nc.tensor.matmul_mx(
-                        acc[:, half, :],
-                        lhsT=w2_codes[:, half, w_cols].bitcast(FP8X4),
-                        lhsT_scale=w2_scales[:, w_cols],
-                        rhs=codes.bitcast(FP8X4),
-                        rhs_scale=scales,
-                        start=(a == 0 and half == 0),
-                        stop=(a == 1 and half == 1),
-                    )
-            result = tile([P, 2, P], F32, f"result{j}")
-            copy = nc.scalar.copy if j % 2 == 0 else nc.vector.tensor_copy
-            copy(result[:], acc[:])
-            nc.sync.dma_start(out_stripes[:, j], result[:])
+            z_codes, z_scales = quantize(z_bf[:].rearrange("p c t -> p (c t)"), f"z{c}")
+            acc = psum([P, CHUNK], f"bank{c}")
+            nc.tensor.matmul_mx(
+                acc[:],
+                lhsT=w2_codes[:].bitcast(FP8X4),
+                lhsT_scale=w2_scales[:],
+                rhs=z_codes[:].bitcast(FP8X4),
+                rhs_scale=z_scales[:],
+                start=True,
+                stop=True,
+            )
+            result = tile([P, CHUNK], F32, f"result{c}")
+            nc.scalar.copy(result[:], acc[:])
+            nc.sync.dma_start(out[:, CHUNK * c : CHUNK * (c + 1)], result[:])

@@ -21,7 +21,8 @@ K_PASS = 4 * P
 LIST_ROWS = 16
 HEAD_S = 256
 CHUNK = 256
-CAST_V = 80
+SHARE_S = 128
+CAST_V = 64
 
 
 def tile_picked_unet_gelu_p_kernel(
@@ -32,8 +33,8 @@ def tile_picked_unet_gelu_p_kernel(
         sb = ctx.enter_context(tc.tile_pool(name="sb", bufs=1))
         ps = ctx.enter_context(tc.psum_pool(name="ps", bufs=1))
 
-        def tile(shape, dtype, name, tag=None):
-            return sb.tile(shape, dtype, name=name, tag=tag or name, align_bytes=64)
+        def tile(shape, dtype, name, tag=None, pool=sb):
+            return pool.tile(shape, dtype, name=name, tag=tag or name, align_bytes=64)
 
         def psum(shape, tag):
             return ps.tile(shape, F32, name=tag, tag=tag)
@@ -47,24 +48,28 @@ def tile_picked_unet_gelu_p_kernel(
         nc.sync.dma_start(cell_sb[:], cell)
 
         x_scales_sb = tile([P, T], U8, "x_scales_sb", "chain")
-        nc.gpsimd.memset(x_scales_sb[:].bitcast(I32), 0)
-        for q in range(4):
-            nc.sync.dma_start(
-                x_scales_sb[32 * q : 32 * q + 8, :].bitcast(I32),
-                x_scales[:, 4 * q : 4 * q + 4, :].bitcast(I32),
+        nc.vector.memset(x_scales_sb[:].bitcast(I32), 0)
+        nc.sync.dma_start(x_scales_sb[0:P:4, :].bitcast(I32), x_scales.rearrange("g b c -> b g c").bitcast(I32))
+
+        up = [tile([P, U], F32, f"up{t}") for t in range(4)]
+        with tc.tile_pool(name="early", bufs=1) as early:
+            zeros = tile([P, 16], F32, "zeros", pool=early)
+            nc.vector.memset(zeros[:], 0.0)
+            nc.vector.tensor_copy(
+                up[0][:].rearrange("p (a b) -> p a b", b=16), zeros[:].unsqueeze(1).to_broadcast([P, U // 16, 16])
             )
+        late = ctx.enter_context(tc.tile_pool(name="late", bufs=1))
+        pools = (sb, late)
 
         w1_raw, x_words_sb = [], []
         for g in range(2):
-            raw = tile([P, 4, H], F32, f"w1_raw{g}", f"raw{g}")
+            raw = tile([P, 4, H], F32, f"w1_raw{g}", f"raw{g}", pools[g])
             nc.sync.dma_start(raw[:], w1[K_PASS * g : K_PASS * (g + 1), :].rearrange("(p s) c -> p s c", s=4))
             w1_raw.append(raw)
-            words = tile([P, T], I32, f"x_words{g}")
+            words = tile([P, T], I32, f"x_words{g}", pool=late)
             nc.sync.dma_start(words[:], x_words[g].rearrange("p n s -> p (n s)").bitcast(I32))
             x_words_sb.append(words)
 
-        up = [tile([P, U], F32, f"up{t}") for t in range(4)]
-        nc.vector.memset(up[0][:], 0.0)
         nc.scalar.copy(up[2][:], up[0][:])
         nc.vector.memset(up[1][:], 0.0)
         nc.vector.memset(up[3][:], 0.0)
@@ -82,10 +87,18 @@ def tile_picked_unet_gelu_p_kernel(
                 raw[:].rearrange("p s (m t) -> p m s t", t=4)[:, m0:m1],
             )
 
+        picked_rows = tile([P, S], U8, "picked_rows")
+        nc.vector.tensor_copy(picked_rows[:], x_scales_sb[:].indirect(offs_sb[:]))
         picked_scales = tile([P, S], U8, "picked_scales")
-        nc.vector.tensor_copy(picked_scales[:], x_scales_sb[:].indirect(offs_sb[:]))
+        nc.vector.tensor_copy(picked_scales[:].bitcast(I32), picked_rows[:].bitcast(I32))
+        for r in range(1, 4):
+            for g in range(2):
+                nc.scalar.dma_start(
+                    picked_scales[4 * g + r : P : 32, :].bitcast(I32), picked_rows[8 * r + 4 * g : P : 32, :].bitcast(I32)
+                )
         w1_bf0 = tile([P, 4, P, 4], BF16, "w1_bf0", "bf0")
-        cast_w1(nc.vector.tensor_copy, w1_bf0, w1_raw[0], 0, P)
+        cast_w1(nc.vector.tensor_copy, w1_bf0, w1_raw[0], 0, CAST_V)
+        cast_w1(nc.scalar.copy, w1_bf0, w1_raw[0], CAST_V, P)
         w1_q = [quantize(w1_bf0[:].rearrange("p t m s -> p (t m s)"), "w1_q0")]
         picked_words = [tile([P, S], U32, "picked_words0")]
         nc.vector.tensor_copy(picked_words[0][:], x_words_sb[0][:].bitcast(U32).indirect(offs_sb[:]))
@@ -100,13 +113,18 @@ def tile_picked_unet_gelu_p_kernel(
             )
 
         skip_rows = skip.rearrange("(p t) v -> p t v", t=4)
+        w2_raw = tile([P, 4, N], F32, "w2_raw", "raw0")
+        nc.sync.dma_start(w2_raw[:], w2.rearrange("(p s) m -> p s m", s=4))
         skip_sb = []
-        for u in range(2):
-            pair = tile([P, 2, U], F32, f"skip{u}", f"raw{u}")
+        for u, tag in enumerate(("bf0", "raw1")):
+            pair = tile([P, 2, U], F32, f"skip{u}", tag, pools[u])
             nc.sync.dma_start(pair[:], skip_rows[:, 2 * u : 2 * u + 2, :])
             skip_sb.append(pair)
-        w2_raw = tile([P, 4, N], F32, "w2_raw", "bf0")
-        nc.sync.dma_start(w2_raw[:], w2.rearrange("(p s) m -> p s m", s=4))
+        w2_bf = tile([P, N, 4], BF16, "w2_bf")
+        nc.vector.tensor_copy(
+            w2_bf[:].rearrange("p (c n) s -> p c s n", n=4), w2_raw[:].rearrange("p s (c n) -> p c s n", n=4)
+        )
+        w2_codes, w2_scales = quantize(w2_bf[:].rearrange("p m s -> p (m s)"), "w2")
 
         pieces = [(0, (0, HEAD_S)), (0, (HEAD_S, S))] + [(t, (0, S)) for t in range(1, 4)]
         banks = [psum([P, b[-1] - b[0]], f"bank{n}") for n, (t, b) in enumerate(pieces)]
@@ -129,13 +147,19 @@ def tile_picked_unet_gelu_p_kernel(
             h_sb = tile([P, bounds[-1] - bounds[0]], F32, f"h{n}")
             nc.scalar.activation(h_sb[:], bank[:], GELU)
             h.append(h_sb)
-        for h_sb, (t, bounds) in zip(h, pieces):
-            if t < 2:
-                nc.vector.tensor_copy(up[t][:].indirect(entries(cell_sb, bounds[0], bounds[-1])), h_sb[:])
-            else:
-                for lo in (0, S // 2):
-                    hi = lo + S // 2
-                    nc.scalar.activation(up[t][:].indirect(entries(cell_sb, lo, hi)), h_sb[:, lo:hi], COPY)
+        def scatter_v(t, lo, hi, src):
+            nc.vector.tensor_copy(up[t][:].indirect(entries(cell_sb, lo, hi)), src)
+
+        def scatter_s(t, lo, hi, src):
+            nc.scalar.activation(up[t][:].indirect(entries(cell_sb, lo, hi)), src, COPY)
+
+        scatter_v(0, 0, HEAD_S, h[0][:])
+        scatter_v(0, HEAD_S, S, h[1][:])
+        scatter_s(1, 0, SHARE_S, h[2][:, :SHARE_S])
+        scatter_v(1, SHARE_S, S, h[2][:, SHARE_S:])
+        for t in (2, 3):
+            for lo in (0, S // 2):
+                scatter_s(t, lo, lo + S // 2, h[t + 1][:, lo : lo + S // 2])
 
         chunks = range(U // CHUNK)
         planes = [tile([P, 4, CHUNK], BF16, f"planes{c}") for c in chunks]
@@ -147,22 +171,19 @@ def tile_picked_unet_gelu_p_kernel(
         for t in range(2):
             for c in chunks:
                 add_skip(t, c)
-        w2_bf = tile([P, N, 4], BF16, "w2_bf")
-        nc.vector.tensor_copy(
-            w2_bf[:].rearrange("p (c n) s -> p c s n", n=4), w2_raw[:].rearrange("p s (c n) -> p c s n", n=4)
-        )
         for c in chunks:
             add_skip(2, c)
-            add_skip(3, c)
-        w2_codes, w2_scales = quantize(w2_bf[:].rearrange("p m s -> p (m s)"), "w2")
-
         for c in chunks:
-            z_bf = tile([P, CHUNK, 4], BF16, f"z_bf{c}")
+            add_skip(3, c)
+
+        z_bf = [tile([P, CHUNK, 4], BF16, f"z_bf{c}") for c in chunks]
+        for c in chunks:
             copy = nc.scalar.copy if c < 2 else nc.vector.tensor_copy
             copy(
-                z_bf[:].rearrange("p (c n) t -> p c t n", n=4), planes[c][:].rearrange("p t (c n) -> p c t n", n=4)
+                z_bf[c][:].rearrange("p (c n) t -> p c t n", n=4), planes[c][:].rearrange("p t (c n) -> p c t n", n=4)
             )
-            z_codes, z_scales = quantize(z_bf[:].rearrange("p c t -> p (c t)"), f"z{c}")
+        for c in (0, 2, 3, 1):
+            z_codes, z_scales = quantize(z_bf[c][:].rearrange("p c t -> p (c t)"), f"z{c}")
             acc = psum([P, CHUNK], f"bank{c}")
             nc.tensor.matmul_mx(
                 acc[:],
@@ -174,5 +195,6 @@ def tile_picked_unet_gelu_p_kernel(
                 stop=True,
             )
             result = tile([P, CHUNK], F32, f"result{c}")
-            nc.scalar.copy(result[:], acc[:])
+            copy = nc.vector.tensor_copy if c == 1 else nc.scalar.copy
+            copy(result[:], acc[:])
             nc.sync.dma_start(out[:, CHUNK * c : CHUNK * (c + 1)], result[:])

@@ -21,8 +21,9 @@ K_PASS = 4 * P
 LIST_ROWS = 16
 HEAD_S = 256
 CHUNK = 256
+BLOCK = 128
 SHARE_S = 128
-CAST_V = 64
+CAST_V = 80
 
 
 def tile_picked_unet_gelu_p_kernel(
@@ -126,7 +127,7 @@ def tile_picked_unet_gelu_p_kernel(
         )
         w2_codes, w2_scales = quantize(w2_bf[:].rearrange("p m s -> p (m s)"), "w2")
 
-        pieces = [(0, (0, HEAD_S)), (0, (HEAD_S, S))] + [(t, (0, S)) for t in range(1, 4)]
+        pieces = [(0, (0, 128)), (1, (0, 256)), (0, (128, 256, S)), (1, (384, S)), (2, (0, S)), (3, (0, S)), (1, (256, 384))]
         banks = [psum([P, b[-1] - b[0]], f"bank{n}") for n, (t, b) in enumerate(pieces)]
         for g in range(2):
             codes, scales = w1_q[g]
@@ -143,48 +144,56 @@ def tile_picked_unet_gelu_p_kernel(
                         stop=(g == 1 and hi == bounds[-1]),
                     )
         h = []
-        for n, (bank, (t, bounds)) in enumerate(zip(banks, pieces)):
-            h_sb = tile([P, bounds[-1] - bounds[0]], F32, f"h{n}")
+        for n, bank in enumerate(banks):
+            h_sb = tile([P, bank.shape[1]], F32, f"h{n}")
             nc.scalar.activation(h_sb[:], bank[:], GELU)
             h.append(h_sb)
+
         def scatter_v(t, lo, hi, src):
             nc.vector.tensor_copy(up[t][:].indirect(entries(cell_sb, lo, hi)), src)
 
         def scatter_s(t, lo, hi, src):
             nc.scalar.activation(up[t][:].indirect(entries(cell_sb, lo, hi)), src, COPY)
 
-        scatter_v(0, 0, HEAD_S, h[0][:])
-        scatter_v(0, HEAD_S, S, h[1][:])
-        scatter_s(1, 0, SHARE_S, h[2][:, :SHARE_S])
-        scatter_v(1, SHARE_S, S, h[2][:, SHARE_S:])
-        for t in (2, 3):
-            for lo in (0, S // 2):
-                scatter_s(t, lo, lo + S // 2, h[t + 1][:, lo : lo + S // 2])
+        scatter_v(0, 0, 128, h[0][:])
+        scatter_v(1, 0, 256, h[1][:])
+        scatter_v(0, 128, S, h[2][:])
+        scatter_s(1, 256, 384, h[6][:])
+        scatter_v(1, 384, S, h[3][:])
+        for lo in (0, S // 2):
+            for t in (2, 3):
+                scatter_s(t, lo, lo + S // 2, h[t + 2][:, lo : lo + S // 2])
 
-        chunks = range(U // CHUNK)
-        planes = [tile([P, 4, CHUNK], BF16, f"planes{c}") for c in chunks]
+        planes = tile([P, U // BLOCK, 4, BLOCK], BF16, "planes")
 
-        def add_skip(t, c):
-            cells = slice(CHUNK * c, CHUNK * (c + 1))
-            nc.vector.tensor_tensor(planes[c][:, t, :], up[t][:, cells], skip_sb[t // 2][:, t % 2, cells], ADD)
-
-        for t in range(2):
-            for c in chunks:
-                add_skip(t, c)
-        for c in chunks:
-            add_skip(2, c)
-        for c in chunks:
-            add_skip(3, c)
-
-        z_bf = [tile([P, CHUNK, 4], BF16, f"z_bf{c}") for c in chunks]
-        for c in chunks:
-            copy = nc.scalar.copy if c < 2 else nc.vector.tensor_copy
-            copy(
-                z_bf[c][:].rearrange("p (c n) t -> p c t n", n=4), planes[c][:].rearrange("p t (c n) -> p c t n", n=4)
+        def add_skip(t, lo, hi):
+            nc.vector.tensor_tensor(
+                planes[:, lo // BLOCK : hi // BLOCK, t, :],
+                up[t][:, lo:hi].rearrange("p (b v) -> p b v", v=BLOCK),
+                skip_sb[t // 2][:, t % 2, lo:hi].rearrange("p (b v) -> p b v", v=BLOCK),
+                ADD,
             )
-        for c in (0, 2, 3, 1):
-            z_codes, z_scales = quantize(z_bf[c][:].rearrange("p c t -> p (c t)"), f"z{c}")
-            acc = psum([P, CHUNK], f"bank{c}")
+
+        for t in range(3):
+            add_skip(t, 0, U)
+        for lo in range(0, U, CHUNK):
+            add_skip(3, lo, lo + CHUNK)
+
+        z_bf = tile([P, U, 4], BF16, "z_bf")
+
+        def interleave(copy, lo, hi):
+            for at in range(lo, hi, BLOCK):
+                copy(
+                    z_bf[:, at : at + BLOCK].rearrange("p (c n) t -> p c t n", n=4),
+                    planes[:, at // BLOCK].rearrange("p t (c n) -> p c t n", n=4),
+                )
+
+        interleave(nc.scalar.copy, 0, U // 2)
+        interleave(nc.vector.tensor_copy, U // 2, U)
+        stretches = [(0, 256), (512, 768), (768, 1024), (256, 384), (384, 512)]
+        for n, (lo, hi) in enumerate(stretches):
+            z_codes, z_scales = quantize(z_bf[:, lo:hi].rearrange("p c t -> p (c t)"), f"z{n}")
+            acc = psum([P, hi - lo], f"bank{n}")
             nc.tensor.matmul_mx(
                 acc[:],
                 lhsT=w2_codes[:].bitcast(FP8X4),
@@ -194,7 +203,7 @@ def tile_picked_unet_gelu_p_kernel(
                 start=True,
                 stop=True,
             )
-            result = tile([P, CHUNK], F32, f"result{c}")
-            copy = nc.vector.tensor_copy if c == 1 else nc.scalar.copy
+            result = tile([P, hi - lo], F32, f"result{n}")
+            copy = nc.scalar.copy if n < 4 else nc.vector.tensor_copy
             copy(result[:], acc[:])
-            nc.sync.dma_start(out[:, CHUNK * c : CHUNK * (c + 1)], result[:])
+            nc.sync.dma_start(out[:, lo:hi], result[:])

@@ -71,7 +71,7 @@ def tile_picked_unet_gelu_p_kernel(
             nc.sync.dma_start(words[:], x_words[g].rearrange("p n s -> p (n s)").bitcast(I32))
             x_words_sb.append(words)
 
-        nc.scalar.copy(up[2][:], up[0][:])
+        nc.scalar.activation(up[2][:], up[0][:], GELU)
         nc.vector.memset(up[1][:], 0.0)
         nc.vector.memset(up[3][:], 0.0)
 

@@ -56,9 +56,7 @@ def tile_picked_unet_gelu_p_kernel(
         with tc.tile_pool(name="early", bufs=1) as early:
             zeros = tile([P, 16], F32, "zeros", pool=early)
             nc.vector.memset(zeros[:], 0.0)
-            nc.vector.tensor_copy(
-                up[0][:].rearrange("p (a b) -> p a b", b=16), zeros[:].unsqueeze(1).to_broadcast([P, U // 16, 16])
-            )
+            nc.vector.tensor_copy(up[0][:, 0:16], zeros[:])
         late = ctx.enter_context(tc.tile_pool(name="late", bufs=1))
         pools = (sb, late)
 
@@ -71,6 +69,7 @@ def tile_picked_unet_gelu_p_kernel(
             nc.sync.dma_start(words[:], x_words[g].rearrange("p n s -> p (n s)").bitcast(I32))
             x_words_sb.append(words)
 
+        nc.vector.memset(up[0][:, 16:U], 0.0)
         nc.scalar.activation(up[2][:], up[0][:], GELU)
         nc.vector.memset(up[1][:], 0.0)
         nc.vector.memset(up[3][:], 0.0)

@@ -126,7 +126,7 @@ def tile_picked_unet_gelu_p_kernel(
         )
         w2_codes, w2_scales = quantize(w2_bf[:].rearrange("p m s -> p (m s)"), "w2")
 
-        pieces = [(0, (0, 128)), (1, (0, 256)), (0, (128, 256, S)), (1, (384, S)), (2, (0, S)), (3, (0, S)), (1, (256, 384))]
+        pieces = [(0, (0, 128)), (0, (128, 256, S)), (2, (0, S)), (1, (0, S)), (3, (0, S))]
         banks = [psum([P, b[-1] - b[0]], f"bank{n}") for n, (t, b) in enumerate(pieces)]
         for g in range(2):
             codes, scales = w1_q[g]
@@ -155,26 +155,28 @@ def tile_picked_unet_gelu_p_kernel(
             nc.scalar.activation(up[t][:].indirect(entries(cell_sb, lo, hi)), src, COPY)
 
         scatter_v(0, 0, 128, h[0][:])
-        scatter_v(1, 0, 256, h[1][:])
-        scatter_v(0, 128, S, h[2][:])
-        scatter_s(1, 256, 384, h[6][:])
-        scatter_v(1, 384, S, h[3][:])
-        for lo in (0, S // 2):
-            for t in (2, 3):
-                scatter_s(t, lo, lo + S // 2, h[t + 2][:, lo : lo + S // 2])
+        scatter_v(0, 128, S, h[1][:])
+        scatter_v(1, 0, S, h[3][:])
+        for t, n in ((2, 2), (3, 4)):
+            for lo in (0, S // 2):
+                scatter_s(t, lo, lo + S // 2, h[n][:, lo : lo + S // 2])
 
         planes = tile([P, U // BLOCK, 4, BLOCK], BF16, "planes")
 
-        def add_skip(t, lo, hi):
-            nc.vector.tensor_tensor(
+        def add_skip(t, lo, hi, engine=nc.vector):
+            engine.tensor_tensor(
                 planes[:, lo // BLOCK : hi // BLOCK, t, :],
                 up[t][:, lo:hi].rearrange("p (b v) -> p b v", v=BLOCK),
                 skip_sb[t // 2][:, t % 2, lo:hi].rearrange("p (b v) -> p b v", v=BLOCK),
                 ADD,
             )
 
-        for t in range(3):
-            add_skip(t, 0, U)
+        for lo in range(0, U, CHUNK):
+            add_skip(0, lo, lo + CHUNK, nc.gpsimd)
+        for lo in range(0, U // 2, CHUNK):
+            add_skip(2, lo, lo + CHUNK, nc.gpsimd)
+        add_skip(1, 0, U)
+        add_skip(2, U // 2, U)
         for lo in range(0, U, CHUNK):
             add_skip(3, lo, lo + CHUNK)
 

@@ -126,7 +126,7 @@ def tile_picked_unet_gelu_p_kernel(
         )
         w2_codes, w2_scales = quantize(w2_bf[:].rearrange("p m s -> p (m s)"), "w2")
 
-        pieces = [(0, (0, 128)), (0, (128, 256, S)), (2, (0, S)), (1, (0, S)), (3, (0, S))]
+        pieces = [(0, (0, 128)), (1, (0, 128)), (0, (128, 256, S)), (2, (0, S)), (1, (128, 256, S)), (3, (0, S))]
         banks = [psum([P, b[-1] - b[0]], f"bank{n}") for n, (t, b) in enumerate(pieces)]
         for g in range(2):
             codes, scales = w1_q[g]
@@ -155,11 +155,13 @@ def tile_picked_unet_gelu_p_kernel(
             nc.scalar.activation(up[t][:].indirect(entries(cell_sb, lo, hi)), src, COPY)
 
         scatter_v(0, 0, 128, h[0][:])
-        scatter_v(0, 128, S, h[1][:])
-        scatter_v(1, 0, S, h[3][:])
-        for t, n in ((2, 2), (3, 4)):
-            for lo in (0, S // 2):
-                scatter_s(t, lo, lo + S // 2, h[n][:, lo : lo + S // 2])
+        scatter_v(1, 0, 128, h[1][:])
+        scatter_v(0, 128, S, h[2][:])
+        scatter_v(1, 128, S, h[4][:])
+        scatter_s(2, 0, 256, h[3][:, 0:256])
+        scatter_s(3, 0, 256, h[5][:, 0:256])
+        scatter_s(2, 256, S, h[3][:, 256:S])
+        scatter_s(3, 256, S, h[5][:, 256:S])
 
         planes = tile([P, U // BLOCK, 4, BLOCK], BF16, "planes")
 
@@ -171,12 +173,9 @@ def tile_picked_unet_gelu_p_kernel(
                 ADD,
             )
 
-        for lo in range(0, U, CHUNK):
-            add_skip(0, lo, lo + CHUNK, nc.gpsimd)
-        for lo in range(0, U // 2, CHUNK):
-            add_skip(2, lo, lo + CHUNK, nc.gpsimd)
+        add_skip(0, 0, U, nc.gpsimd)
+        add_skip(2, 0, U)
         add_skip(1, 0, U)
-        add_skip(2, U // 2, U)
         for lo in range(0, U, CHUNK):
             add_skip(3, lo, lo + CHUNK)
 

@@ -15,11 +15,12 @@ FP8X4 = mybir.dt.float8_e4m3fn_x4
 GELU = mybir.ActivationFunctionType.Gelu_apprx_tanh
 COPY = mybir.ActivationFunctionType.Copy
 ADD = mybir.AluOpType.add
+MULT = mybir.AluOpType.mult
 
 P = 128
 K_PASS = 4 * P
 LIST_ROWS = 16
-HEAD_S = 256
+HEAD_S = 128
 CHUNK = 256
 BLOCK = 128
 SHARE_S = 128
@@ -121,9 +122,7 @@ def tile_picked_unet_gelu_p_kernel(
             nc.sync.dma_start(pair[:], skip_rows[:, 2 * u : 2 * u + 2, :])
             skip_sb.append(pair)
         w2_bf = tile([P, N, 4], BF16, "w2_bf")
-        nc.vector.tensor_copy(
-            w2_bf[:].rearrange("p (c n) s -> p c s n", n=4), w2_raw[:].rearrange("p s (c n) -> p c s n", n=4)
-        )
+        nc.gpsimd.tensor_scalar(w2_bf[:], w2_raw[:].rearrange("p s m -> p m s"), 1.0, 0.0, MULT, ADD)
         w2_codes, w2_scales = quantize(w2_bf[:].rearrange("p m s -> p (m s)"), "w2")
 
         pieces = [(0, (0, 128)), (1, (0, 128)), (0, (128, 256, S)), (2, (0, S)), (1, (128, 256, S)), (3, (0, S))]

from contextlib import ExitStack

import concourse.mybir as mybir

K, T, S, H, N, U = 1024, 2048, 512, 512, 128, 1024
FLOPS = 2 * K * H * S + 2 * H * N * U

F32 = mybir.dt.float32
BF16 = mybir.dt.bfloat16
I32 = mybir.dt.int32
U32 = mybir.dt.uint32
U16 = mybir.dt.uint16
U8 = mybir.dt.uint8
FP8X4 = mybir.dt.float8_e4m3fn_x4
GELU = mybir.ActivationFunctionType.Gelu_apprx_tanh
COPY = mybir.ActivationFunctionType.Copy
ADD = mybir.AluOpType.add
MULT = mybir.AluOpType.mult

P = 128
K_PASS = 4 * P
LIST_ROWS = 16
HEAD_S = 128
CHUNK = 256
BLOCK = 128
SHARE_S = 128
CAST_V = 80


def tile_picked_unet_gelu_p_kernel(
    tc, x_words, x_scales, w1, w2, skip, offs, cell, out
):
    nc = tc.nc
    with ExitStack() as ctx:
        sb = ctx.enter_context(tc.tile_pool(name="sb", bufs=1))
        ps = ctx.enter_context(tc.psum_pool(name="ps", bufs=1))

        def tile(shape, dtype, name, tag=None, pool=sb):
            return pool.tile(shape, dtype, name=name, tag=tag or name, align_bytes=64)

        def psum(shape, tag):
            return ps.tile(shape, F32, name=tag, tag=tag)

        def entries(list_sb, lo, hi):
            return list_sb[:, lo // LIST_ROWS : hi // LIST_ROWS]

        offs_sb = tile([P, S // LIST_ROWS], U16, "offs_sb")
        cell_sb = tile([P, S // LIST_ROWS], U16, "cell_sb")
        nc.sync.dma_start(offs_sb[:], offs)
        nc.sync.dma_start(cell_sb[:], cell)

        x_scales_sb = tile([P, T], U8, "x_scales_sb", "chain")
        nc.vector.memset(x_scales_sb[:].bitcast(I32), 0)
        nc.sync.dma_start(x_scales_sb[0:P:4, :].bitcast(I32), x_scales.rearrange("g b c -> b g c").bitcast(I32))

        up = [tile([P, U], F32, f"up{t}") for t in range(4)]
        with tc.tile_pool(name="early", bufs=1) as early:
            zeros = tile([P, 16], F32, "zeros", pool=early)
            nc.vector.memset(zeros[:], 0.0)
            nc.vector.tensor_copy(up[0][:, 0:16], zeros[:])
        late = ctx.enter_context(tc.tile_pool(name="late", bufs=1))
        pools = (sb, late)

        w1_raw, x_words_sb = [], []
        for g in range(2):
            raw = tile([P, 4, H], F32, f"w1_raw{g}", f"raw{g}", pools[g])
            nc.sync.dma_start(raw[:], w1[K_PASS * g : K_PASS * (g + 1), :].rearrange("(p s) c -> p s c", s=4))
            w1_raw.append(raw)
            words = tile([P, T], I32, f"x_words{g}", pool=late)
            nc.sync.dma_start(words[:], x_words[g].rearrange("p n s -> p (n s)").bitcast(I32))
            x_words_sb.append(words)

        nc.vector.memset(up[0][:, 16:U], 0.0)
        nc.scalar.activation(up[2][:], up[0][:], GELU)
        nc.vector.memset(up[1][:], 0.0)
        nc.vector.memset(up[3][:], 0.0)

        def quantize(src, name):
            width = src.shape[1] // 4
            codes = tile([P, width], U32, name + "_codes")
            scales = tile([P, width], U8, name + "_scales")
            nc.vector.quantize_mx(out=codes[:].bitcast(FP8X4), scales=scales[:], in_=src)
            return codes, scales

        def cast_w1(copy, grouped, raw, m0, m1):
            copy(
                grouped[:, :, m0:m1, :].rearrange("p t m s -> p m s t"),
                raw[:].rearrange("p s (m t) -> p m s t", t=4)[:, m0:m1],
            )

        picked_rows = tile([P, S], U8, "picked_rows")
        nc.vector.tensor_copy(picked_rows[:], x_scales_sb[:].indirect(offs_sb[:]))
        picked_scales = tile([P, S], U8, "picked_scales")
        nc.vector.tensor_copy(picked_scales[:].bitcast(I32), picked_rows[:].bitcast(I32))
        for r in range(1, 4):
            for g in range(2):
                nc.scalar.dma_start(
                    picked_scales[4 * g + r : P : 32, :].bitcast(I32), picked_rows[8 * r + 4 * g : P : 32, :].bitcast(I32)
                )
        w1_bf0 = tile([P, 4, P, 4], BF16, "w1_bf0", "bf0")
        cast_w1(nc.vector.tensor_copy, w1_bf0, w1_raw[0], 0, CAST_V)
        cast_w1(nc.scalar.copy, w1_bf0, w1_raw[0], CAST_V, P)
        w1_q = [quantize(w1_bf0[:].rearrange("p t m s -> p (t m s)"), "w1_q0")]
        picked_words = [tile([P, S], U32, "picked_words0")]
        nc.vector.tensor_copy(picked_words[0][:], x_words_sb[0][:].bitcast(U32).indirect(offs_sb[:]))
        w1_bf1 = tile([P, 4, P, 4], BF16, "w1_bf1", "chain")
        cast_w1(nc.vector.tensor_copy, w1_bf1, w1_raw[1], 0, CAST_V)
        cast_w1(nc.scalar.copy, w1_bf1, w1_raw[1], CAST_V, P)
        w1_q.append(quantize(w1_bf1[:].rearrange("p t m s -> p (t m s)"), "w1_q1"))
        picked_words.append(tile([P, S], U32, "picked_words1", "chain"))
        for lo, hi in ((0, HEAD_S), (HEAD_S, S)):
            nc.vector.tensor_copy(
                picked_words[1][:, lo:hi], x_words_sb[1][:].bitcast(U32).indirect(entries(offs_sb, lo, hi))
            )

        skip_rows = skip.rearrange("(p t) v -> p t v", t=4)
        w2_raw = tile([P, 4, N], F32, "w2_raw", "raw0")
        nc.sync.dma_start(w2_raw[:], w2.rearrange("(p s) m -> p s m", s=4))
        skip_sb = []
        for u, tag in enumerate(("bf0", "raw1")):
            pair = tile([P, 2, U], F32, f"skip{u}", tag, pools[u])
            nc.sync.dma_start(pair[:], skip_rows[:, 2 * u : 2 * u + 2, :])
            skip_sb.append(pair)
        w2_bf = tile([P, N, 4], BF16, "w2_bf")
        nc.gpsimd.tensor_scalar(w2_bf[:], w2_raw[:].rearrange("p s m -> p m s"), 1.0, 0.0, MULT, ADD)
        w2_codes, w2_scales = quantize(w2_bf[:].rearrange("p m s -> p (m s)"), "w2")

        pieces = [(0, (0, 128)), (1, (0, 128)), (0, (128, 256, S)), (2, (0, S)), (1, (128, 256, S)), (3, (0, S))]
        banks = [psum([P, b[-1] - b[0]], f"bank{n}") for n, (t, b) in enumerate(pieces)]
        for g in range(2):
            codes, scales = w1_q[g]
            for bank, (t, bounds) in zip(banks, pieces):
                cols = slice(P * t, P * (t + 1))
                for lo, hi in zip(bounds, bounds[1:]):
                    nc.tensor.matmul_mx(
                        bank[:, lo - bounds[0] : hi - bounds[0]],
                        lhsT=codes[:, cols].bitcast(FP8X4),
                        lhsT_scale=scales[:, cols],
                        rhs=picked_words[g][:, lo:hi].bitcast(FP8X4),
                        rhs_scale=picked_scales[4 * g :, lo:hi],
                        start=(g == 0 and lo == bounds[0]),
                        stop=(g == 1 and hi == bounds[-1]),
                    )
        h = []
        for n, bank in enumerate(banks):
            h_sb = tile([P, bank.shape[1]], F32, f"h{n}")
            nc.scalar.activation(h_sb[:], bank[:], GELU)
            h.append(h_sb)

        def scatter_v(t, lo, hi, src):
            nc.vector.tensor_copy(up[t][:].indirect(entries(cell_sb, lo, hi)), src)

        def scatter_s(t, lo, hi, src):
            nc.scalar.activation(up[t][:].indirect(entries(cell_sb, lo, hi)), src, COPY)

        scatter_v(0, 0, 128, h[0][:])
        scatter_v(1, 0, 128, h[1][:])
        scatter_v(0, 128, S, h[2][:])
        scatter_v(1, 128, S, h[4][:])
        scatter_s(2, 0, 256, h[3][:, 0:256])
        scatter_s(3, 0, 256, h[5][:, 0:256])
        scatter_s(2, 256, S, h[3][:, 256:S])
        scatter_s(3, 256, S, h[5][:, 256:S])

        planes = tile([P, U // BLOCK, 4, BLOCK], BF16, "planes")

        def add_skip(t, lo, hi, engine=nc.vector):
            engine.tensor_tensor(
                planes[:, lo // BLOCK : hi // BLOCK, t, :],
                up[t][:, lo:hi].rearrange("p (b v) -> p b v", v=BLOCK),
                skip_sb[t // 2][:, t % 2, lo:hi].rearrange("p (b v) -> p b v", v=BLOCK),
                ADD,
            )

        add_skip(0, 0, U, nc.gpsimd)
        add_skip(2, 0, U)
        add_skip(1, 0, U)
        for lo in range(0, U, CHUNK):
            add_skip(3, lo, lo + CHUNK)

        z_bf = tile([P, U, 4], BF16, "z_bf")

        def interleave(copy, lo, hi):
            for at in range(lo, hi, BLOCK):
                copy(
                    z_bf[:, at : at + BLOCK].rearrange("p (c n) t -> p c t n", n=4),
                    planes[:, at // BLOCK].rearrange("p t (c n) -> p c t n", n=4),
                )

        interleave(nc.scalar.copy, 0, U // 2)
        interleave(nc.vector.tensor_copy, U // 2, U)
        stretches = [(0, 256), (512, 768), (768, 1024), (256, 384), (384, 512)]
        for n, (lo, hi) in enumerate(stretches):
            z_codes, z_scales = quantize(z_bf[:, lo:hi].rearrange("p c t -> p (c t)"), f"z{n}")
            acc = psum([P, hi - lo], f"bank{n}")
            nc.tensor.matmul_mx(
                acc[:],
                lhsT=w2_codes[:].bitcast(FP8X4),
                lhsT_scale=w2_scales[:],
                rhs=z_codes[:].bitcast(FP8X4),
                rhs_scale=z_scales[:],
                start=True,
                stop=True,
            )
            result = tile([P, hi - lo], F32, f"result{n}")
            copy = nc.scalar.copy if n < 4 else nc.vector.tensor_copy
            copy(result[:], acc[:])
            nc.sync.dma_start(out[:, lo:hi], result[:])
